import numpy as np
import ml_dtypes


def mxq(x, axis, fmt="e4m3"):
    dtype, down = {"e4m3": (ml_dtypes.float8_e4m3fn, 7), "e5m2": (ml_dtypes.float8_e5m2, 14)}[fmt]
    v = np.moveaxis(np.asarray(x, np.float32).astype(ml_dtypes.bfloat16).astype(np.float64), axis, -1)
    blocks = v.reshape(v.shape[:-1] + (-1, 32))
    amax = np.abs(blocks).max(-1, keepdims=True)
    byte = np.maximum(np.where(amax > 0, np.frexp(amax)[1] - 1 + 127, 0) - down, 1)
    scale = np.exp2(byte - 127.0)
    codes = (blocks / scale).astype(np.float32).astype(dtype).astype(np.float64)
    return np.moveaxis((codes * scale).reshape(v.shape), -1, axis)


WIDE = False


def mx_kscale(k):
    if not WIDE:
        return np.ones(k)
    levels = np.array([10, -10, 5, -5, 0])
    if k % 512:
        return np.exp2(np.random.permutation(np.resize(levels, k // 32))).repeat(32)
    a = np.empty((k // 512, 16))
    for p in range(k // 512):
        a[p, :8] = np.random.permutation(np.resize(levels, 8))
        for g in range(8):
            far = levels[np.abs(levels - a[p, g]) >= 10]
            a[p, g + 8] = far[np.random.randint(len(far))]
    return np.exp2(a.ravel()).repeat(32)


def f64(x):
    return np.asarray(x).astype(np.float64)


def striped(idx):
    return np.tile(idx.reshape(-1, 16).T, (8, 1)).astype(np.uint16)


def unstriped(offs):
    return offs[:16].T.reshape(-1).astype(np.int64)


def pack_weight(w):
    k, n = w.shape
    w = f64(np.asarray(w, np.float32).astype(ml_dtypes.bfloat16)).reshape(k // 32, 32, n)
    amax = np.abs(w).max(1)
    byte = np.clip(np.where(amax > 0, np.frexp(amax)[1] - 1 + 127 - 7, 1), 1, 254)
    scaled = (w * np.exp2(127.0 - byte)[:, None, :]).reshape(k, n).astype(np.float32)
    words = np.ascontiguousarray(scaled.reshape(k // 512, 128, 4, n).transpose(0, 1, 3, 2)).astype(ml_dtypes.float8_e4m3fn).view(np.uint8)
    return words, np.ascontiguousarray(byte.astype(np.uint8).reshape(k // 512, 16, n))


def unpack_weight(words, scales):
    g, p, n, _ = words.shape
    vals = np.ascontiguousarray(words).view(ml_dtypes.float8_e4m3fn).astype(np.float64) * np.repeat(np.exp2(scales.astype(np.float64) - 127.0), 8, axis=1)[..., None]
    return vals.transpose(0, 1, 3, 2).reshape(g * 512, n)


def relu(v):
    return np.maximum(v, 0.0)


K, T, S, H, N, U = 1024, 2048, 512, 512, 128, 1024


def setup_inputs():
    n = np.random.standard_normal
    s = mx_kscale(K)[:, None]
    u = mx_kscale(H)
    packed_xT = pack_weight(n((K, T)) * s)
    return {
        "x_words": packed_xT[0],
        "x_scales": packed_xT[1],
        "w1": (n((K, H)) / np.sqrt(K) / s * u).astype(np.float32),
        "w2": (n((H, N)) / np.sqrt(H) / u[:, None]).astype(np.float32),
        "skip": (n((H, U)) * u[:, None]).astype(np.float32),
        "offs": striped(np.random.permutation(T)[:S]),
        "cell": striped(np.random.permutation(U)[:S]),
    }


def reference(x_words, x_scales, w1, w2, skip, offs, cell):
    xq = unpack_weight(x_words, x_scales)[:, unstriped(offs)]
    up = np.zeros((H, U))
    up[:, unstriped(cell)] = relu(mxq(f64(w1), 0, "e4m3").T @ xq)
    z = up + f64(skip)
    return mxq(f64(w2), 0, "e4m3").T @ mxq(z, 0, "e4m3")

@@ -1,0 +1,223 @@
+from contextlib import ExitStack
+
+import concourse.mybir as mybir
+from concourse.masks import make_identity
+
+K, T, S, H, N, U = 1024, 2048, 512, 512, 128, 1024
+FLOPS = 2 * K * H * S + 2 * H * N * U
+
+F32 = mybir.dt.float32
+BF16 = mybir.dt.bfloat16
+I32 = mybir.dt.int32
+U32 = mybir.dt.uint32
+U16 = mybir.dt.uint16
+U8 = mybir.dt.uint8
+FP8X4 = mybir.dt.float8_e4m3fn_x4
+ACT = mybir.ActivationFunctionType
+
+P = 128
+PASSES = 2
+TILES = 4
+HALF = 64
+
+
+def tile_picked_unet_relu_p_kernel(tc, x_words, x_scales, w1, w2, skip, offs, cell, out):
+    nc = tc.nc
+    with ExitStack() as ctx:
+        sb = ctx.enter_context(tc.tile_pool(name="sb", bufs=1))
+        ps = ctx.enter_context(tc.psum_pool(name="ps", bufs=1))
+
+        offs_t = sb.tile([P, S // 16], U16, name="offs_t")
+        cell_t = sb.tile([P, S // 16], U16, name="cell_t")
+        xs = sb.tile([P, T], U8, name="xs", align_bytes=64)
+        xw = [sb.tile([P, T], I32, name=f"xw{z}", align_bytes=64) for z in range(PASSES)]
+        ident = sb.tile([P, P], F32, name="ident", align_bytes=64)
+
+        nc.vector.memset(xs[:].bitcast(I32), 0)
+        nc.sync.dma_start(offs_t[:], offs)
+        for q in range(4):
+            nc.scalar.dma_start(xs[32 * q : 32 * q + 8, :].bitcast(I32), x_scales[:, 4 * q : 4 * q + 4, :].bitcast(I32))
+
+        w1_raw = {}
+
+        def load_w1(c0, c1):
+            for z in range(PASSES):
+                raw = sb.tile([P, 4, c1 - c0], F32, name=f"w1raw{c0}_{z}", tag=f"raw{c0 // P}_{z}", align_bytes=64)
+                nc.sync.dma_start(raw[:], w1[512 * z : 512 * (z + 1), c0:c1].rearrange("(p j) c -> p j c", j=4))
+                for t in range(c0 // P, c1 // P):
+                    w1_raw[t, z] = raw[:, :, t * P - c0 : (t + 1) * P - c0]
+
+        load_w1(0, 128)
+        for z in range(PASSES):
+            nc.sync.dma_start(xw[z][:], x_words[z].rearrange("p n t -> p (n t)").bitcast(I32))
+        nc.sync.dma_start(cell_t[:], cell)
+        load_w1(128, 256)
+        load_w1(256, 384)
+        load_w1(384, 512)
+        skip_t = []
+        w2_raw = sb.tile([P, 2, 4 * N], F32, name="w2raw", align_bytes=64)
+        for t in range(TILES):
+            sk = sb.tile([P, U], F32, name=f"skip{t}", align_bytes=64)
+            nc.sync.dma_start(sk[:], skip[P * t : P * (t + 1), :])
+            skip_t.append(sk)
+            if t == 1:
+                for hf in range(2):
+                    nc.sync.dma_start(w2_raw[HALF * hf : HALF * (hf + 1)], w2.rearrange("(g r j) n -> r g (j n)", g=2, j=4))
+
+        make_identity(nc, ident[:])
+        window = []
+        for t in range(TILES):
+            win = sb.tile([P, U], F32, name=f"window{t}", align_bytes=64)
+            nc.vector.memset(win[:], 0.0)
+            window.append(win)
+        w2_b = sb.tile([P, 2, 2, N, 4], BF16, name="w2b", align_bytes=64)
+        nc.gpsimd.memset(w2_b[:].rearrange("p g h n j -> p (g h n j)").bitcast(I32), 0)
+
+        w1_codes, w1_scales = {}, {}
+
+        def quantise_w1(t):
+            wb = sb.tile([P, PASSES, P, 4], BF16, name=f"w1b{t}", align_bytes=64)
+            for z in range(PASSES):
+                nc.scalar.activation(
+                    out=wb[:, z].rearrange("p (c i) j -> p c j i", i=4),
+                    in_=w1_raw[t, z].rearrange("p j (c i) -> p c j i", i=4),
+                    func=ACT.Copy,
+                )
+            codes = sb.tile([P, PASSES * P], U32, name=f"w1c{t}", align_bytes=64)
+            scales = sb.tile([P, PASSES * P], U8, name=f"w1s{t}", align_bytes=64)
+            nc.vector.quantize_mx(out=codes[:].bitcast(FP8X4), scales=scales[:], in_=wb[:].rearrange("p z c j -> p (z c j)"))
+            w1_codes[t], w1_scales[t] = codes, scales
+
+        gs = sb.tile([P, S], U8, name="gs", align_bytes=64)
+        gw = [sb.tile([P, S], U32, name=f"gw{z}", align_bytes=64) for z in range(PASSES)]
+
+        def gather_words(z, j0, j1):
+            nc.vector.tensor_copy(gw[z][:, j0:j1], xw[z][:].bitcast(U32).indirect(offs_t[:, j0 // 16 : j1 // 16]))
+
+        banks = ["acc0", "acc1", "acc2", "acc3"]
+
+        def first_layer(t, j0, j1, bank, slot):
+            acc = ps.tile([P, j1 - j0], F32, name=f"h{t}_{j0}", tag=bank)
+            for z in range(PASSES):
+                nc.tensor.matmul_mx(
+                    out=acc[:],
+                    lhsT=w1_codes[t][:, P * z : P * (z + 1)].bitcast(FP8X4),
+                    lhsT_scale=w1_scales[t][:, P * z : P * (z + 1)],
+                    rhs=gw[z][:, j0:j1].bitcast(FP8X4),
+                    rhs_scale=gs[4 * z : P, j0:j1],
+                    start=(z == 0),
+                    stop=(z == PASSES - 1),
+                )
+            h = sb.tile([P, j1 - j0], F32, name=f"hs{t}_{j0}", tag=slot, align_bytes=64)
+            nc.scalar.activation(out=h[:], in_=acc[:], func=ACT.Relu)
+            return h
+
+        def scatter(t, j0, j1, h):
+            nc.vector.tensor_copy(window[t][:].indirect(cell_t[:, j0 // 16 : j1 // 16]), h[:])
+
+        zt = {}
+        for g in range(2):
+            for c in range(4):
+                zt[g, c] = sb.tile([P, 512], BF16, name=f"zt{g}_{c}", align_bytes=64)
+
+        def turn_and_add(t):
+            g, tl = divmod(t, 2)
+            zbank = []
+            for k in range(2):
+                zb = ps.tile([P, 2, 2, P], F32, name=f"zb{t}_{k}", tag=f"turn{k}")
+                zbank.append(zb)
+                for n, (cl, hf) in enumerate([(a, b) for a in range(2) for b in range(2)]):
+                    v0 = 512 * hf + P * (2 * k + cl)
+                    nc.tensor.matmul(zb[:, cl, hf, :], skip_t[t][:, v0 : v0 + P], ident[:], start=(n == 0), stop=False, is_transpose=True)
+            for k in range(2):
+                zb = zbank[k]
+                for n, (cl, hf) in enumerate([(a, b) for a in range(2) for b in range(2)]):
+                    v0 = 512 * hf + P * (2 * k + cl)
+                    nc.tensor.matmul(zb[:, cl, hf, :], window[t][:, v0 : v0 + P], ident[:], start=False, stop=(n == 3), is_transpose=True)
+                for cl in range(2):
+                    dst = zt[g, 2 * k + cl][:].rearrange("p (u h t r e) -> p u h t r e", u=2, h=2, t=2, e=2)[:, :, :, tl]
+                    nc.scalar.copy(dst, zb[:, cl].rearrange("p h (r u e) -> p u h r e", u=2, e=2))
+
+        def turn_back(g, k, tags, copies):
+            grouped = sb.tile([P, 2, 256], F32, name=f"grouped{g}_{k}", align_bytes=64)
+            for cl in range(2):
+                xt = ps.tile([P, 2, P], F32, name=f"xt{g}_{k}_{cl}", tag=tags[cl])
+                words = zt[g, 2 * k + cl][:].bitcast(F32)
+                for u in range(2):
+                    nc.tensor.transpose(xt[:, u, :], words[:, P * u : P * (u + 1)], ident[:])
+                copies[cl](grouped[:, cl].rearrange("p (y u) -> p y u", u=2), xt[:].rearrange("p u y -> p y u"))
+            return grouped
+
+        def quantise_z(grouped, codes, scales):
+            nc.vector.quantize_mx(out=codes.bitcast(FP8X4), scales=scales, in_=grouped[:].rearrange("p c w -> p (c w)").bitcast(BF16))
+            return codes, scales
+
+        nc.vector.tensor_copy(gs[:], xs[:].indirect(offs_t[:]))
+        gather_words(0, 0, S)
+        quantise_w1(0)
+        gather_words(1, 0, 256)
+        h0a = first_layer(0, 0, 256, banks[0], "h0a")
+        gather_words(1, 256, S)
+        scatter(0, 0, 256, h0a)
+        quantise_w1(1)
+        h0b = first_layer(0, 256, S, banks[1], "raw1_1")
+        scatter(0, 256, S, h0b)
+        quantise_w1(2)
+        h1 = first_layer(1, 0, S, banks[2], "raw2_1")
+        scatter(1, 0, S, h1)
+        turn_and_add(0)
+        quantise_w1(3)
+        h2 = first_layer(2, 0, S, banks[3], "raw3_1")
+        h3 = first_layer(3, 0, S, banks[0], "late")
+        scatter(2, 0, S, h2)
+        turn_and_add(1)
+        for hf in range(2):
+            rows = slice(HALF * hf, HALF * (hf + 1))
+            for g in range(2):
+                nc.scalar.activation(
+                    out=w2_b[rows, g, hf].rearrange("p (c i) j -> p c j i", i=4),
+                    in_=w2_raw[rows, g].rearrange("p (j c i) -> p c j i", j=4, i=4),
+                    func=ACT.Copy,
+                )
+        grouped_a = [turn_back(0, k, ["back0", "back1"], [nc.scalar.copy, nc.scalar.copy]) for k in range(2)]
+        scatter(3, 0, S, h3)
+        turn_and_add(2)
+        turn_and_add(3)
+
+        late_codes = sb.tile([P, 1024], U32, name="late_codes", tag="late", align_bytes=64)
+        w2_codes = late_codes[:, 512:1024]
+        w2_scales = sb.tile([P, 4 * N], U8, name="w2s", align_bytes=64)
+        nc.vector.quantize_mx(out=w2_codes.bitcast(FP8X4), scales=w2_scales[:], in_=w2_b[:].rearrange("p g h n j -> p (g h n j)"))
+        za_scales = sb.tile([P, 512], U8, name="zas", align_bytes=64)
+        z_a = [quantise_z(grouped_a[k], late_codes[:, 256 * k : 256 * (k + 1)], za_scales[:, 256 * k : 256 * (k + 1)]) for k in range(2)]
+
+        both = [nc.scalar.copy, nc.vector.tensor_copy]
+        grouped_b = [turn_back(1, 0, ["back0", "back1"], both), turn_back(1, 1, ["turn0", "turn1"], both)]
+
+        def second_layer(acc, g, hf, z):
+            cols = slice(N * (2 * g + hf), N * (2 * g + hf + 1))
+            nc.tensor.matmul_mx(
+                out=acc[:],
+                lhsT=w2_codes[:, cols].bitcast(FP8X4),
+                lhsT_scale=w2_scales[:, cols],
+                rhs=z[0].bitcast(FP8X4),
+                rhs_scale=z[1],
+                start=(g == 0),
+                stop=(g == 1),
+            )
+
+        accs = {}
+        for k in range(2):
+            for hf in range(2):
+                accs[k, hf] = ps.tile([P, 256], F32, name=f"o{k}_{hf}", tag=banks[2 * k + hf])
+                second_layer(accs[k, hf], 0, hf, z_a[k])
+        for k in range(2):
+            codes = sb.tile([P, 256], U32, name=f"zc{k}", align_bytes=64)
+            scales = sb.tile([P, 256], U8, name=f"zs{k}", align_bytes=64)
+            z_b = quantise_z(grouped_b[k], codes[:], scales[:])
+            for hf in range(2):
+                second_layer(accs[k, hf], 1, hf, z_b)
+                res = sb.tile([P, 256], F32, name=f"res{k}_{hf}", align_bytes=64)
+                both[hf](res[:], accs[k, hf][:])
+                v0 = 512 * hf + 256 * k
+                nc.sync.dma_start(out[:, v0 : v0 + 256], res[:])

@@ -33,10 +33,16 @@ def tile_picked_unet_relu_p_kernel(tc, x_words, x_scales, w1, w2, skip, offs, ce
         xw = [sb.tile([P, T], I32, name=f"xw{z}", align_bytes=64) for z in range(PASSES)]
         ident = sb.tile([P, P], F32, name="ident", align_bytes=64)
 
-        nc.vector.memset(xs[:].bitcast(I32), 0)
+        nc.gpsimd.memset(xs[:].bitcast(I32), 0)
         nc.sync.dma_start(offs_t[:], offs)
+        nc.sync.dma_start(cell_t[:], cell)
+
+        def load_words(z):
+            nc.sync.dma_start(xw[z][:], x_words[z].rearrange("p n t -> p (n t)").bitcast(I32))
+
+        load_words(0)
         for q in range(4):
-            nc.scalar.dma_start(xs[32 * q : 32 * q + 8, :].bitcast(I32), x_scales[:, 4 * q : 4 * q + 4, :].bitcast(I32))
+            nc.sync.dma_start(xs[32 * q : 32 * q + 8, :].bitcast(I32), x_scales[:, 4 * q : 4 * q + 4, :].bitcast(I32))
 
         w1_raw = {}
 
@@ -48,9 +54,7 @@ def tile_picked_unet_relu_p_kernel(tc, x_words, x_scales, w1, w2, skip, offs, ce
                     w1_raw[t, z] = raw[:, :, t * P - c0 : (t + 1) * P - c0]
 
         load_w1(0, 128)
-        for z in range(PASSES):
-            nc.sync.dma_start(xw[z][:], x_words[z].rearrange("p n t -> p (n t)").bitcast(I32))
-        nc.sync.dma_start(cell_t[:], cell)
+        load_words(1)
         load_w1(128, 256)
         load_w1(256, 384)
         load_w1(384, 512)
@@ -76,11 +80,11 @@ def tile_picked_unet_relu_p_kernel(tc, x_words, x_scales, w1, w2, skip, offs, ce
         w1_codes, w1_scales = {}, {}
 
         def quantise_w1(t):
-            wb = sb.tile([P, PASSES, P, 4], BF16, name=f"w1b{t}", align_bytes=64)
+            wb = sb.tile([P, PASSES, P, 4], BF16, name=f"w1b{t}", tag=f"w1b{t}", align_bytes=64)
             for z in range(PASSES):
                 nc.scalar.activation(
-                    out=wb[:, z].rearrange("p (c i) j -> p c j i", i=4),
-                    in_=w1_raw[t, z].rearrange("p j (c i) -> p c j i", i=4),
+                    out=wb[:, z],
+                    in_=w1_raw[t, z].rearrange("p j c -> p c j"),
                     func=ACT.Copy,
                 )
             codes = sb.tile([P, PASSES * P], U32, name=f"w1c{t}", align_bytes=64)
@@ -89,7 +93,7 @@ def tile_picked_unet_relu_p_kernel(tc, x_words, x_scales, w1, w2, skip, offs, ce
             w1_codes[t], w1_scales[t] = codes, scales
 
         gs = sb.tile([P, S], U8, name="gs", align_bytes=64)
-        gw = [sb.tile([P, S], U32, name=f"gw{z}", align_bytes=64) for z in range(PASSES)]
+        gw = {}
 
         def gather_words(z, j0, j1):
             nc.vector.tensor_copy(gw[z][:, j0:j1], xw[z][:].bitcast(U32).indirect(offs_t[:, j0 // 16 : j1 // 16]))
@@ -120,23 +124,24 @@ def tile_picked_unet_relu_p_kernel(tc, x_words, x_scales, w1, w2, skip, offs, ce
             for c in range(4):
                 zt[g, c] = sb.tile([P, 512], BF16, name=f"zt{g}_{c}", align_bytes=64)
 
-        def turn_and_add(t):
+        def turn_and_add(t, groups, copies):
             g, tl = divmod(t, 2)
             zbank = []
-            for k in range(2):
-                zb = ps.tile([P, 2, 2, P], F32, name=f"zb{t}_{k}", tag=f"turn{k}")
+            for tag, cs in groups:
+                zb = ps.tile([P, len(cs), 2, P], F32, name=f"zb{t}_{tag}", tag=tag)
                 zbank.append(zb)
-                for n, (cl, hf) in enumerate([(a, b) for a in range(2) for b in range(2)]):
-                    v0 = 512 * hf + P * (2 * k + cl)
-                    nc.tensor.matmul(zb[:, cl, hf, :], skip_t[t][:, v0 : v0 + P], ident[:], start=(n == 0), stop=False, is_transpose=True)
-            for k in range(2):
-                zb = zbank[k]
-                for n, (cl, hf) in enumerate([(a, b) for a in range(2) for b in range(2)]):
-                    v0 = 512 * hf + P * (2 * k + cl)
-                    nc.tensor.matmul(zb[:, cl, hf, :], window[t][:, v0 : v0 + P], ident[:], start=False, stop=(n == 3), is_transpose=True)
-                for cl in range(2):
-                    dst = zt[g, 2 * k + cl][:].rearrange("p (u h t r e) -> p u h t r e", u=2, h=2, t=2, e=2)[:, :, :, tl]
-                    nc.scalar.copy(dst, zb[:, cl].rearrange("p h (r u e) -> p u h r e", u=2, e=2))
+                blocks = [(n, c, hf) for n, c in enumerate(cs) for hf in range(2)]
+                for n, c, hf in blocks:
+                    v0 = 512 * hf + P * c
+                    nc.tensor.matmul(zb[:, n, hf, :], skip_t[t][:, v0 : v0 + P], ident[:], start=(n == 0 and hf == 0), stop=False, is_transpose=True)
+            for zb, (tag, cs) in zip(zbank, groups):
+                blocks = [(n, c, hf) for n, c in enumerate(cs) for hf in range(2)]
+                for n, c, hf in blocks:
+                    v0 = 512 * hf + P * c
+                    nc.tensor.matmul(zb[:, n, hf, :], window[t][:, v0 : v0 + P], ident[:], start=False, stop=(n == len(cs) - 1 and hf == 1), is_transpose=True)
+                for n, c in enumerate(cs):
+                    dst = zt[g, c][:].rearrange("p (u h t r e) -> p u h t r e", u=2, h=2, t=2, e=2)[:, :, :, tl]
+                    copies[c](dst, zb[:, n].rearrange("p h (r u e) -> p u h r e", u=2, e=2))
 
         def turn_back(g, k, tags, copies):
             grouped = sb.tile([P, 2, 256], F32, name=f"grouped{g}_{k}", align_bytes=64)
@@ -152,9 +157,14 @@ def tile_picked_unet_relu_p_kernel(tc, x_words, x_scales, w1, w2, skip, offs, ce
             nc.vector.quantize_mx(out=codes.bitcast(FP8X4), scales=scales, in_=grouped[:].rearrange("p c w -> p (c w)").bitcast(BF16))
             return codes, scales
 
+        act, dve = nc.scalar.copy, nc.vector.tensor_copy
+        two_banks = [("turn0", (0, 1)), ("turn1", (2, 3))]
+        four_banks = [(banks[c], (c,)) for c in range(4)]
         nc.vector.tensor_copy(gs[:], xs[:].indirect(offs_t[:]))
+        gw[0] = sb.tile([P, S], U32, name="gw0", align_bytes=64)
         gather_words(0, 0, S)
         quantise_w1(0)
+        gw[1] = sb.tile([P, S], U32, name="gw1", tag="w1b0", align_bytes=64)
         gather_words(1, 0, 256)
         h0a = first_layer(0, 0, 256, banks[0], "h0a")
         gather_words(1, 256, S)
@@ -165,24 +175,24 @@ def tile_picked_unet_relu_p_kernel(tc, x_words, x_scales, w1, w2, skip, offs, ce
         quantise_w1(2)
         h1 = first_layer(1, 0, S, banks[2], "raw2_1")
         scatter(1, 0, S, h1)
-        turn_and_add(0)
+        turn_and_add(0, two_banks, [act] * 4)
         quantise_w1(3)
         h2 = first_layer(2, 0, S, banks[3], "raw3_1")
         h3 = first_layer(3, 0, S, banks[0], "late")
         scatter(2, 0, S, h2)
-        turn_and_add(1)
+        turn_and_add(1, two_banks, [act] * 4)
         for hf in range(2):
             rows = slice(HALF * hf, HALF * (hf + 1))
             for g in range(2):
                 nc.scalar.activation(
-                    out=w2_b[rows, g, hf].rearrange("p (c i) j -> p c j i", i=4),
-                    in_=w2_raw[rows, g].rearrange("p (j c i) -> p c j i", j=4, i=4),
+                    out=w2_b[rows, g, hf],
+                    in_=w2_raw[rows, g].rearrange("p (j c) -> p c j", j=4),
                     func=ACT.Copy,
                 )
         grouped_a = [turn_back(0, k, ["back0", "back1"], [nc.scalar.copy, nc.scalar.copy]) for k in range(2)]
         scatter(3, 0, S, h3)
-        turn_and_add(2)
-        turn_and_add(3)
+        turn_and_add(2, two_banks, [act] * 4)
+        turn_and_add(3, four_banks, [act, act, act, dve])
 
         late_codes = sb.tile([P, 1024], U32, name="late_codes", tag="late", align_bytes=64)
         w2_codes = late_codes[:, 512:1024]
@@ -192,7 +202,8 @@ def tile_picked_unet_relu_p_kernel(tc, x_words, x_scales, w1, w2, skip, offs, ce
         z_a = [quantise_z(grouped_a[k], late_codes[:, 256 * k : 256 * (k + 1)], za_scales[:, 256 * k : 256 * (k + 1)]) for k in range(2)]
 
         both = [nc.scalar.copy, nc.vector.tensor_copy]
-        grouped_b = [turn_back(1, 0, ["back0", "back1"], both), turn_back(1, 1, ["turn0", "turn1"], both)]
+        last_banks = ["back0", "back1", "turn0", "turn1"]
+        grouped_b = [turn_back(1, 0, last_banks[:2], [act, dve]), turn_back(1, 1, last_banks[2:], [act, act])]
 
         def second_layer(acc, g, hf, z):
             cols = slice(N * (2 * g + hf), N * (2 * g + hf + 1))
@@ -209,7 +220,7 @@ def tile_picked_unet_relu_p_kernel(tc, x_words, x_scales, w1, w2, skip, offs, ce
         accs = {}
         for k in range(2):
             for hf in range(2):
-                accs[k, hf] = ps.tile([P, 256], F32, name=f"o{k}_{hf}", tag=banks[2 * k + hf])
+                accs[k, hf] = ps.tile([P, 256], F32, name=f"o{k}_{hf}", tag=last_banks[2 * k + hf])
                 second_layer(accs[k, hf], 0, hf, z_a[k])
         for k in range(2):
             codes = sb.tile([P, 256], U32, name=f"zc{k}", align_bytes=64)

@@ -56,17 +56,21 @@ def tile_picked_unet_relu_p_kernel(tc, x_words, x_scales, w1, w2, skip, offs, ce
         load_w1(0, 128)
         load_words(1)
         load_w1(128, 256)
+        skip_t = {}
+
+        def load_skip(t):
+            skip_t[t] = sb.tile([P, U], F32, name=f"skip{t}", align_bytes=64)
+            nc.sync.dma_start(skip_t[t][:], skip[P * t : P * (t + 1), :])
+
         load_w1(256, 384)
         load_w1(384, 512)
-        skip_t = []
+        load_skip(0)
         w2_raw = sb.tile([P, 2, 4 * N], F32, name="w2raw", align_bytes=64)
-        for t in range(TILES):
-            sk = sb.tile([P, U], F32, name=f"skip{t}", align_bytes=64)
-            nc.sync.dma_start(sk[:], skip[P * t : P * (t + 1), :])
-            skip_t.append(sk)
-            if t == 1:
-                for hf in range(2):
-                    nc.sync.dma_start(w2_raw[HALF * hf : HALF * (hf + 1)], w2.rearrange("(g r j) n -> r g (j n)", g=2, j=4))
+        for hf in range(2):
+            nc.sync.dma_start(w2_raw[HALF * hf : HALF * (hf + 1)], w2.rearrange("(g r j) n -> r g (j n)", g=2, j=4))
+        load_skip(1)
+        load_skip(2)
+        load_skip(3)
 
         make_identity(nc, ident[:])
         window = []
@@ -74,8 +78,8 @@ def tile_picked_unet_relu_p_kernel(tc, x_words, x_scales, w1, w2, skip, offs, ce
             win = sb.tile([P, U], F32, name=f"window{t}", align_bytes=64)
             nc.vector.memset(win[:], 0.0)
             window.append(win)
-        w2_b = sb.tile([P, 2, 2, N, 4], BF16, name="w2b", align_bytes=64)
-        nc.gpsimd.memset(w2_b[:].rearrange("p g h n j -> p (g h n j)").bitcast(I32), 0)
+        w2_masked = sb.tile([P, 2, 2, N], I32, name="w2m", align_bytes=64)
+        nc.gpsimd.memset(w2_masked[:], 0)
 
         w1_codes, w1_scales = {}, {}
 
@@ -120,9 +124,6 @@ def tile_picked_unet_relu_p_kernel(tc, x_words, x_scales, w1, w2, skip, offs, ce
             nc.vector.tensor_copy(window[t][:].indirect(cell_t[:, j0 // 16 : j1 // 16]), h[:])
 
         zt = {}
-        for g in range(2):
-            for c in range(4):
-                zt[g, c] = sb.tile([P, 512], BF16, name=f"zt{g}_{c}", align_bytes=64)
 
         def turn_and_add(t, groups, copies):
             g, tl = divmod(t, 2)
@@ -140,14 +141,14 @@ def tile_picked_unet_relu_p_kernel(tc, x_words, x_scales, w1, w2, skip, offs, ce
                     v0 = 512 * hf + P * c
                     nc.tensor.matmul(zb[:, n, hf, :], window[t][:, v0 : v0 + P], ident[:], start=False, stop=(n == len(cs) - 1 and hf == 1), is_transpose=True)
                 for n, c in enumerate(cs):
-                    dst = zt[g, c][:].rearrange("p (u h t r e) -> p u h t r e", u=2, h=2, t=2, e=2)[:, :, :, tl]
+                    dst = zt[g, c].rearrange("p (u h t r e) -> p u h t r e", u=2, h=2, t=2, e=2)[:, :, :, tl]
                     copies[c](dst, zb[:, n].rearrange("p h (r u e) -> p u h r e", u=2, e=2))
 
         def turn_back(g, k, tags, copies):
             grouped = sb.tile([P, 2, 256], F32, name=f"grouped{g}_{k}", align_bytes=64)
             for cl in range(2):
                 xt = ps.tile([P, 2, P], F32, name=f"xt{g}_{k}_{cl}", tag=tags[cl])
-                words = zt[g, 2 * k + cl][:].bitcast(F32)
+                words = zt[g, 2 * k + cl].bitcast(F32)
                 for u in range(2):
                     nc.tensor.transpose(xt[:, u, :], words[:, P * u : P * (u + 1)], ident[:])
                 copies[cl](grouped[:, cl].rearrange("p (y u) -> p y u", u=2), xt[:].rearrange("p u y -> p y u"))
@@ -173,62 +174,68 @@ def tile_picked_unet_relu_p_kernel(tc, x_words, x_scales, w1, w2, skip, offs, ce
         h0b = first_layer(0, 256, S, banks[1], "raw1_1")
         scatter(0, 256, S, h0b)
         quantise_w1(2)
-        h1 = first_layer(1, 0, S, banks[2], "raw2_1")
-        scatter(1, 0, S, h1)
-        turn_and_add(0, two_banks, [act] * 4)
+        h1a = first_layer(1, 0, 256, banks[2], "raw2_1")
+        scatter(1, 0, 256, h1a)
         quantise_w1(3)
-        h2 = first_layer(2, 0, S, banks[3], "raw3_1")
-        h3 = first_layer(3, 0, S, banks[0], "late")
+        h1b = first_layer(1, 256, S, banks[3], "raw3_1")
+        scatter(1, 256, S, h1b)
+        h2 = first_layer(2, 0, S, banks[0], "h2")
+        h3 = first_layer(3, 0, S, banks[1], "late")
+        w2_b = sb.tile([P, 2, N, 4], BF16, name="w2b", align_bytes=64)
+        nc.scalar.activation(out=w2_b[:], in_=w2_raw[:].rearrange("p g (j n) -> p g n j", j=4), func=ACT.Copy)
+        zt_a = sb.tile([P, 4 * 512], BF16, name="zt_a", tag="raw3_0", align_bytes=64)
+        for c in range(4):
+            zt[0, c] = zt_a[:, 512 * c : 512 * (c + 1)]
+            zt_b = sb.tile([P, 512], BF16, name=f"zt_b{c}", align_bytes=64)
+            zt[1, c] = zt_b[:]
+        turn_and_add(0, two_banks, [act] * 4)
         scatter(2, 0, S, h2)
         turn_and_add(1, two_banks, [act] * 4)
-        for hf in range(2):
-            rows = slice(HALF * hf, HALF * (hf + 1))
-            for g in range(2):
-                nc.scalar.activation(
-                    out=w2_b[rows, g, hf],
-                    in_=w2_raw[rows, g].rearrange("p (j c) -> p c j", j=4),
-                    func=ACT.Copy,
-                )
         grouped_a = [turn_back(0, k, ["back0", "back1"], [nc.scalar.copy, nc.scalar.copy]) for k in range(2)]
         scatter(3, 0, S, h3)
         turn_and_add(2, two_banks, [act] * 4)
-        turn_and_add(3, four_banks, [act, act, act, dve])
+        turn_and_add(3, four_banks, [act] * 4)
 
-        late_codes = sb.tile([P, 1024], U32, name="late_codes", tag="late", align_bytes=64)
-        w2_codes = late_codes[:, 512:1024]
-        w2_scales = sb.tile([P, 4 * N], U8, name="w2s", align_bytes=64)
-        nc.vector.quantize_mx(out=w2_codes.bitcast(FP8X4), scales=w2_scales[:], in_=w2_b[:].rearrange("p g h n j -> p (g h n j)"))
+        late_codes = sb.tile([P, 768], U32, name="late_codes", tag="late", align_bytes=64)
+        w2_codes = late_codes[:, 512:768]
+        w2_scales = sb.tile([P, 2 * N], U8, name="w2s", align_bytes=64)
+        nc.vector.quantize_mx(out=w2_codes.bitcast(FP8X4), scales=w2_scales[:], in_=w2_b[:].rearrange("p g n j -> p (g n j)"))
         za_scales = sb.tile([P, 512], U8, name="zas", align_bytes=64)
         z_a = [quantise_z(grouped_a[k], late_codes[:, 256 * k : 256 * (k + 1)], za_scales[:, 256 * k : 256 * (k + 1)]) for k in range(2)]
+        for hf in range(2):
+            rows = slice(HALF * hf, HALF * (hf + 1))
+            nc.vector.tensor_copy(w2_masked[rows, :, hf, :], late_codes[rows, 512:768].bitcast(I32).rearrange("p (g n) -> p g n", g=2))
 
         both = [nc.scalar.copy, nc.vector.tensor_copy]
         last_banks = ["back0", "back1", "turn0", "turn1"]
         grouped_b = [turn_back(1, 0, last_banks[:2], [act, dve]), turn_back(1, 1, last_banks[2:], [act, act])]
 
-        def second_layer(acc, g, hf, z):
-            cols = slice(N * (2 * g + hf), N * (2 * g + hf + 1))
+        def second_layer(acc, g, hf, z, start, stop):
             nc.tensor.matmul_mx(
-                out=acc[:],
-                lhsT=w2_codes[:, cols].bitcast(FP8X4),
-                lhsT_scale=w2_scales[:, cols],
+                out=acc,
+                lhsT=w2_masked[:, g, hf, :].bitcast(FP8X4),
+                lhsT_scale=w2_scales[:, N * g : N * (g + 1)],
                 rhs=z[0].bitcast(FP8X4),
                 rhs_scale=z[1],
-                start=(g == 0),
-                stop=(g == 1),
+                start=start,
+                stop=stop,
             )
 
         accs = {}
         for k in range(2):
             for hf in range(2):
                 accs[k, hf] = ps.tile([P, 256], F32, name=f"o{k}_{hf}", tag=last_banks[2 * k + hf])
-                second_layer(accs[k, hf], 0, hf, z_a[k])
+                second_layer(accs[k, hf][:], 0, hf, z_a[k], True, False)
         for k in range(2):
             codes = sb.tile([P, 256], U32, name=f"zc{k}", align_bytes=64)
             scales = sb.tile([P, 256], U8, name=f"zs{k}", align_bytes=64)
-            z_b = quantise_z(grouped_b[k], codes[:], scales[:])
+            for cl in range(2):
+                cols = slice(P * cl, P * (cl + 1))
+                nc.vector.quantize_mx(out=codes[:, cols].bitcast(FP8X4), scales=scales[:, cols], in_=grouped_b[k][:, cl].bitcast(BF16))
+                for hf in range(2):
+                    second_layer(accs[k, hf][:, cols], 1, hf, (codes[:, cols], scales[:, cols]), False, cl == 1)
             for hf in range(2):
-                second_layer(accs[k, hf], 1, hf, z_b)
                 res = sb.tile([P, 256], F32, name=f"res{k}_{hf}", align_bytes=64)
                 both[hf](res[:], accs[k, hf][:])
                 v0 = 512 * hf + 256 * k
-                nc.sync.dma_start(out[:, v0 : v0 + 256], res[:])
+                (nc.scalar if hf == 0 else nc.sync).dma_start(out[:, v0 : v0 + 256], res[:])

@@ -14,6 +14,8 @@ U16 = mybir.dt.uint16
 U8 = mybir.dt.uint8
 FP8X4 = mybir.dt.float8_e4m3fn_x4
 ACT = mybir.ActivationFunctionType
+MULT = mybir.AluOpType.mult
+ADD = mybir.AluOpType.add
 
 P = 128
 PASSES = 2
@@ -65,11 +67,11 @@ def tile_picked_unet_relu_p_kernel(tc, x_words, x_scales, w1, w2, skip, offs, ce
         load_w1(256, 384)
         load_w1(384, 512)
         load_skip(0)
+        load_skip(1)
+        load_skip(2)
         w2_raw = sb.tile([P, 2, 4 * N], F32, name="w2raw", align_bytes=64)
         for hf in range(2):
             nc.sync.dma_start(w2_raw[HALF * hf : HALF * (hf + 1)], w2.rearrange("(g r j) n -> r g (j n)", g=2, j=4))
-        load_skip(1)
-        load_skip(2)
         load_skip(3)
 
         make_identity(nc, ident[:])
@@ -78,8 +80,8 @@ def tile_picked_unet_relu_p_kernel(tc, x_words, x_scales, w1, w2, skip, offs, ce
             win = sb.tile([P, U], F32, name=f"window{t}", align_bytes=64)
             nc.vector.memset(win[:], 0.0)
             window.append(win)
-        w2_masked = sb.tile([P, 2, 2, N], I32, name="w2m", align_bytes=64)
-        nc.gpsimd.memset(w2_masked[:], 0)
+        w2_masked = sb.tile([P, 2, 2, N, 4], BF16, name="w2m", align_bytes=64)
+        nc.gpsimd.memset(w2_masked[:], 0.0)
 
         w1_codes, w1_scales = {}, {}
 
@@ -117,7 +119,10 @@ def tile_picked_unet_relu_p_kernel(tc, x_words, x_scales, w1, w2, skip, offs, ce
                     stop=(z == PASSES - 1),
                 )
             h = sb.tile([P, j1 - j0], F32, name=f"hs{t}_{j0}", tag=slot, align_bytes=64)
-            nc.scalar.activation(out=h[:], in_=acc[:], func=ACT.Relu)
+            if (t, j0) == (0, 0):
+                nc.vector.tensor_scalar_max(h[:], acc[:], 0.0)
+            else:
+                nc.scalar.activation(out=h[:], in_=acc[:], func=ACT.Relu)
             return h
 
         def scatter(t, j0, j1, h):
@@ -144,19 +149,12 @@ def tile_picked_unet_relu_p_kernel(tc, x_words, x_scales, w1, w2, skip, offs, ce
                     dst = zt[g, c].rearrange("p (u h t r e) -> p u h t r e", u=2, h=2, t=2, e=2)[:, :, :, tl]
                     copies[c](dst, zb[:, n].rearrange("p h (r u e) -> p u h r e", u=2, e=2))
 
-        def turn_back(g, k, tags, copies):
-            grouped = sb.tile([P, 2, 256], F32, name=f"grouped{g}_{k}", align_bytes=64)
-            for cl in range(2):
-                xt = ps.tile([P, 2, P], F32, name=f"xt{g}_{k}_{cl}", tag=tags[cl])
-                words = zt[g, 2 * k + cl].bitcast(F32)
-                for u in range(2):
-                    nc.tensor.transpose(xt[:, u, :], words[:, P * u : P * (u + 1)], ident[:])
-                copies[cl](grouped[:, cl].rearrange("p (y u) -> p y u", u=2), xt[:].rearrange("p u y -> p y u"))
-            return grouped
-
-        def quantise_z(grouped, codes, scales):
-            nc.vector.quantize_mx(out=codes.bitcast(FP8X4), scales=scales, in_=grouped[:].rearrange("p c w -> p (c w)").bitcast(BF16))
-            return codes, scales
+        def turn_back(g, c, tag, copy, grouped):
+            xt = ps.tile([P, 2, P], F32, name=f"xt{g}_{c}", tag=tag)
+            words = zt[g, c].bitcast(F32)
+            for u in range(2):
+                nc.tensor.transpose(xt[:, u, :], words[:, P * u : P * (u + 1)], ident[:])
+            copy(grouped.rearrange("p (y u) -> p y u", u=2), xt[:].rearrange("p u y -> p y u"))
 
         act, dve = nc.scalar.copy, nc.vector.tensor_copy
         two_banks = [("turn0", (0, 1)), ("turn1", (2, 3))]
@@ -179,10 +177,11 @@ def tile_picked_unet_relu_p_kernel(tc, x_words, x_scales, w1, w2, skip, offs, ce
         quantise_w1(3)
         h1b = first_layer(1, 256, S, banks[3], "raw3_1")
         scatter(1, 256, S, h1b)
-        h2 = first_layer(2, 0, S, banks[0], "h2")
-        h3 = first_layer(3, 0, S, banks[1], "late")
-        w2_b = sb.tile([P, 2, N, 4], BF16, name="w2b", align_bytes=64)
-        nc.scalar.activation(out=w2_b[:], in_=w2_raw[:].rearrange("p g (j n) -> p g n j", j=4), func=ACT.Copy)
+        h2 = first_layer(2, 0, S, banks[3], "h2")
+        h3a = first_layer(3, 0, 256, banks[3], "late")
+        for hf in range(2):
+            rows = slice(HALF * hf, HALF * (hf + 1))
+            nc.gpsimd.tensor_scalar(w2_masked[rows, :, hf], w2_raw[rows].rearrange("p g (j n) -> p g n j", j=4), 1.0, 0.0, MULT, ADD)
         zt_a = sb.tile([P, 4 * 512], BF16, name="zt_a", tag="raw3_0", align_bytes=64)
         for c in range(4):
             zt[0, c] = zt_a[:, 512 * c : 512 * (c + 1)]
@@ -190,52 +189,64 @@ def tile_picked_unet_relu_p_kernel(tc, x_words, x_scales, w1, w2, skip, offs, ce
             zt[1, c] = zt_b[:]
         turn_and_add(0, two_banks, [act] * 4)
         scatter(2, 0, S, h2)
-        turn_and_add(1, two_banks, [act] * 4)
-        grouped_a = [turn_back(0, k, ["back0", "back1"], [nc.scalar.copy, nc.scalar.copy]) for k in range(2)]
-        scatter(3, 0, S, h3)
-        turn_and_add(2, two_banks, [act] * 4)
-        turn_and_add(3, four_banks, [act] * 4)
+        turn_and_add(1, [("back0", (0, 1)), ("back1", (2, 3))], [act] * 4)
+        grouped_a = sb.tile([P, 4, 256], F32, name="grouped_a", align_bytes=64)
+        for c in range(4):
+            turn_back(0, c, f"back{c % 2}", act, grouped_a[:, c])
+        scatter(3, 0, 256, h3a)
+
+        w2_mx = {}
+
+        def quantise_w2(g, codes):
+            scales = sb.tile([P, 2 * N], U8, name=f"w2s{g}", align_bytes=64)
+            nc.vector.quantize_mx(out=codes.bitcast(FP8X4), scales=scales[:], in_=w2_masked[:, g].rearrange("p h n j -> p (h n j)"))
+            w2_mx[g] = codes, scales
 
         late_codes = sb.tile([P, 768], U32, name="late_codes", tag="late", align_bytes=64)
-        w2_codes = late_codes[:, 512:768]
-        w2_scales = sb.tile([P, 2 * N], U8, name="w2s", align_bytes=64)
-        nc.vector.quantize_mx(out=w2_codes.bitcast(FP8X4), scales=w2_scales[:], in_=w2_b[:].rearrange("p g n j -> p (g n j)"))
+        quantise_w2(0, late_codes[:, 512:768])
         za_scales = sb.tile([P, 512], U8, name="zas", align_bytes=64)
-        z_a = [quantise_z(grouped_a[k], late_codes[:, 256 * k : 256 * (k + 1)], za_scales[:, 256 * k : 256 * (k + 1)]) for k in range(2)]
-        for hf in range(2):
-            rows = slice(HALF * hf, HALF * (hf + 1))
-            nc.vector.tensor_copy(w2_masked[rows, :, hf, :], late_codes[rows, 512:768].bitcast(I32).rearrange("p (g n) -> p g n", g=2))
+        za_codes = late_codes[:, 0:512]
+        nc.vector.quantize_mx(out=za_codes.bitcast(FP8X4), scales=za_scales[:], in_=grouped_a[:].rearrange("p c w -> p (c w)").bitcast(BF16))
+        h3b = first_layer(3, 256, S, banks[2], "raw3_0")
+        scatter(3, 256, S, h3b)
+        turn_and_add(2, two_banks, [act] * 4)
+        w2_last = sb.tile([P, 2 * N], U32, name="w2_last", tag="raw3_0", align_bytes=64)
+        quantise_w2(1, w2_last[:])
+        turn_and_add(3, four_banks, [act, dve, act, dve])
 
-        both = [nc.scalar.copy, nc.vector.tensor_copy]
-        last_banks = ["back0", "back1", "turn0", "turn1"]
-        grouped_b = [turn_back(1, 0, last_banks[:2], [act, dve]), turn_back(1, 1, last_banks[2:], [act, act])]
-
-        def second_layer(acc, g, hf, z, start, stop):
+        def second_layer(acc, g, hf, codes, scales, start, stop):
             nc.tensor.matmul_mx(
                 out=acc,
-                lhsT=w2_masked[:, g, hf, :].bitcast(FP8X4),
-                lhsT_scale=w2_scales[:, N * g : N * (g + 1)],
-                rhs=z[0].bitcast(FP8X4),
-                rhs_scale=z[1],
+                lhsT=w2_mx[g][0][:, N * hf : N * (hf + 1)].bitcast(FP8X4),
+                lhsT_scale=w2_mx[g][1][:, N * hf : N * (hf + 1)],
+                rhs=codes.bitcast(FP8X4),
+                rhs_scale=scales,
                 start=start,
                 stop=stop,
             )
 
+        out_banks = ["back0", "back1", "turn0", "turn1"]
         accs = {}
         for k in range(2):
+            cols = slice(256 * k, 256 * (k + 1))
             for hf in range(2):
-                accs[k, hf] = ps.tile([P, 256], F32, name=f"o{k}_{hf}", tag=last_banks[2 * k + hf])
-                second_layer(accs[k, hf][:], 0, hf, z_a[k], True, False)
+                accs[k, hf] = ps.tile([P, 256], F32, name=f"o{k}_{hf}", tag=out_banks[2 * k + hf])
+                second_layer(accs[k, hf][:], 0, hf, za_codes[:, cols], za_scales[:, cols], True, False)
+        grouped_b = []
+        for c in range(4):
+            grouped = sb.tile([P, 256], F32, name=f"grouped_b{c}", align_bytes=64)
+            turn_back(1, c, banks[c], dve if c == 1 else act, grouped[:])
+            grouped_b.append(grouped)
         for k in range(2):
             codes = sb.tile([P, 256], U32, name=f"zc{k}", align_bytes=64)
             scales = sb.tile([P, 256], U8, name=f"zs{k}", align_bytes=64)
             for cl in range(2):
                 cols = slice(P * cl, P * (cl + 1))
-                nc.vector.quantize_mx(out=codes[:, cols].bitcast(FP8X4), scales=scales[:, cols], in_=grouped_b[k][:, cl].bitcast(BF16))
+                nc.vector.quantize_mx(out=codes[:, cols].bitcast(FP8X4), scales=scales[:, cols], in_=grouped_b[2 * k + cl][:].bitcast(BF16))
                 for hf in range(2):
-                    second_layer(accs[k, hf][:, cols], 1, hf, (codes[:, cols], scales[:, cols]), False, cl == 1)
+                    second_layer(accs[k, hf][:, cols], 1, hf, codes[:, cols], scales[:, cols], False, cl == 1)
             for hf in range(2):
                 res = sb.tile([P, 256], F32, name=f"res{k}_{hf}", align_bytes=64)
-                both[hf](res[:], accs[k, hf][:])
+                (dve if (k, hf) == (1, 1) else act)(res[:], accs[k, hf][:])
                 v0 = 512 * hf + 256 * k
-                (nc.scalar if hf == 0 else nc.sync).dma_start(out[:, v0 : v0 + 256], res[:])
+                nc.sync.dma_start(out[:, v0 : v0 + 256], res[:])

@@ -14,8 +14,6 @@ U16 = mybir.dt.uint16
 U8 = mybir.dt.uint8
 FP8X4 = mybir.dt.float8_e4m3fn_x4
 ACT = mybir.ActivationFunctionType
-MULT = mybir.AluOpType.mult
-ADD = mybir.AluOpType.add
 
 P = 128
 PASSES = 2
@@ -66,13 +64,10 @@ def tile_picked_unet_relu_p_kernel(tc, x_words, x_scales, w1, w2, skip, offs, ce
 
         load_w1(256, 384)
         load_w1(384, 512)
-        load_skip(0)
-        load_skip(1)
-        load_skip(2)
-        w2_raw = sb.tile([P, 2, 4 * N], F32, name="w2raw", align_bytes=64)
-        for hf in range(2):
-            nc.sync.dma_start(w2_raw[HALF * hf : HALF * (hf + 1)], w2.rearrange("(g r j) n -> r g (j n)", g=2, j=4))
-        load_skip(3)
+        w2_raw = sb.tile([P, 4, N], F32, name="w2raw", align_bytes=64)
+        nc.sync.dma_start(w2_raw[:], w2.rearrange("(p j) n -> p j n", j=4))
+        for t in range(TILES):
+            load_skip(t)
 
         make_identity(nc, ident[:])
         window = []
@@ -80,8 +75,10 @@ def tile_picked_unet_relu_p_kernel(tc, x_words, x_scales, w1, w2, skip, offs, ce
             win = sb.tile([P, U], F32, name=f"window{t}", align_bytes=64)
             nc.vector.memset(win[:], 0.0)
             window.append(win)
-        w2_masked = sb.tile([P, 2, 2, N, 4], BF16, name="w2m", align_bytes=64)
-        nc.gpsimd.memset(w2_masked[:], 0.0)
+        w2_masked = sb.tile([P, 2, 2, N], I32, name="w2m", align_bytes=64)
+        nc.gpsimd.memset(w2_masked[:], 0)
+        w2_scales = [sb.tile([P, N], U8, name=f"w2s{s}", align_bytes=64) for s in range(2)]
+        nc.gpsimd.memset(w2_scales[0][:].bitcast(I32), 0)
 
         w1_codes, w1_scales = {}, {}
 
@@ -145,6 +142,10 @@ def tile_picked_unet_relu_p_kernel(tc, x_words, x_scales, w1, w2, skip, offs, ce
                 for n, c, hf in blocks:
                     v0 = 512 * hf + P * c
                     nc.tensor.matmul(zb[:, n, hf, :], window[t][:, v0 : v0 + P], ident[:], start=False, stop=(n == len(cs) - 1 and hf == 1), is_transpose=True)
+                if g == 0:
+                    dst = zt_a[cs[0] // 2][:].rearrange("p c (u h t r e) -> p c h u t r e", u=2, h=2, t=2, e=2)[:, :, :, :, tl]
+                    copies[0](dst, zb[:].rearrange("p c h (r u e) -> p c h u r e", u=2, e=2))
+                    continue
                 for n, c in enumerate(cs):
                     dst = zt[g, c].rearrange("p (u h t r e) -> p u h t r e", u=2, h=2, t=2, e=2)[:, :, :, tl]
                     copies[c](dst, zb[:, n].rearrange("p h (r u e) -> p u h r e", u=2, e=2))
@@ -177,48 +178,47 @@ def tile_picked_unet_relu_p_kernel(tc, x_words, x_scales, w1, w2, skip, offs, ce
         quantise_w1(3)
         h1b = first_layer(1, 256, S, banks[3], "raw3_1")
         scatter(1, 256, S, h1b)
+        w2_b = sb.tile([P, N, 4], BF16, name="w2b", align_bytes=64)
+        nc.scalar.activation(out=w2_b[:], in_=w2_raw[:].rearrange("p j n -> p n j"), func=ACT.Copy)
+        w2_codes = sb.tile([P, N], U32, name="w2c", align_bytes=64)
+        nc.vector.quantize_mx(out=w2_codes[:].bitcast(FP8X4), scales=w2_scales[0][:], in_=w2_b[:].rearrange("p n j -> p (n j)"))
+        halves = [slice(0, HALF), slice(HALF, P)]
+        for g in range(2):
+            for hf in range(2):
+                nc.sync.dma_start(w2_masked[halves[hf], g, hf, :], w2_codes[halves[g], :].bitcast(I32))
+            nc.sync.dma_start(w2_scales[1][halves[1 - g], :].bitcast(I32), w2_scales[0][halves[g], :].bitcast(I32))
         h2 = first_layer(2, 0, S, banks[3], "h2")
         h3a = first_layer(3, 0, 256, banks[3], "late")
-        for hf in range(2):
-            rows = slice(HALF * hf, HALF * (hf + 1))
-            nc.gpsimd.tensor_scalar(w2_masked[rows, :, hf], w2_raw[rows].rearrange("p g (j n) -> p g n j", j=4), 1.0, 0.0, MULT, ADD)
-        zt_a = sb.tile([P, 4 * 512], BF16, name="zt_a", tag="raw3_0", align_bytes=64)
+        zt_a = [sb.tile([P, 2, 512], BF16, name=f"zt_a{k}", tag=f"zt{k}", align_bytes=64) for k in range(2)]
         for c in range(4):
-            zt[0, c] = zt_a[:, 512 * c : 512 * (c + 1)]
             zt_b = sb.tile([P, 512], BF16, name=f"zt_b{c}", align_bytes=64)
             zt[1, c] = zt_b[:]
         turn_and_add(0, two_banks, [act] * 4)
         scatter(2, 0, S, h2)
         turn_and_add(1, [("back0", (0, 1)), ("back1", (2, 3))], [act] * 4)
         grouped_a = sb.tile([P, 4, 256], F32, name="grouped_a", align_bytes=64)
-        for c in range(4):
-            turn_back(0, c, f"back{c % 2}", act, grouped_a[:, c])
+        for k in range(2):
+            xt = ps.tile([P, 2, 2, P], F32, name=f"xt_a{k}", tag=f"back{k}")
+            words = zt_a[k][:].rearrange("p c w -> p (c w)").bitcast(F32)
+            for n in range(4):
+                nc.tensor.transpose(xt[:, n // 2, n % 2, :], words[:, P * n : P * (n + 1)], ident[:])
+            act(grouped_a[:, 2 * k : 2 * k + 2].rearrange("p c (y u) -> p c y u", u=2), xt[:].rearrange("p c u y -> p c y u"))
         scatter(3, 0, 256, h3a)
 
-        w2_mx = {}
-
-        def quantise_w2(g, codes):
-            scales = sb.tile([P, 2 * N], U8, name=f"w2s{g}", align_bytes=64)
-            nc.vector.quantize_mx(out=codes.bitcast(FP8X4), scales=scales[:], in_=w2_masked[:, g].rearrange("p h n j -> p (h n j)"))
-            w2_mx[g] = codes, scales
-
-        late_codes = sb.tile([P, 768], U32, name="late_codes", tag="late", align_bytes=64)
-        quantise_w2(0, late_codes[:, 512:768])
+        late_codes = sb.tile([P, 512], U32, name="late_codes", align_bytes=64)
         za_scales = sb.tile([P, 512], U8, name="zas", align_bytes=64)
         za_codes = late_codes[:, 0:512]
         nc.vector.quantize_mx(out=za_codes.bitcast(FP8X4), scales=za_scales[:], in_=grouped_a[:].rearrange("p c w -> p (c w)").bitcast(BF16))
-        h3b = first_layer(3, 256, S, banks[2], "raw3_0")
+        h3b = first_layer(3, 256, S, banks[2], "zt1")
         scatter(3, 256, S, h3b)
         turn_and_add(2, two_banks, [act] * 4)
-        w2_last = sb.tile([P, 2 * N], U32, name="w2_last", tag="raw3_0", align_bytes=64)
-        quantise_w2(1, w2_last[:])
         turn_and_add(3, four_banks, [act, dve, act, dve])
 
         def second_layer(acc, g, hf, codes, scales, start, stop):
             nc.tensor.matmul_mx(
                 out=acc,
-                lhsT=w2_mx[g][0][:, N * hf : N * (hf + 1)].bitcast(FP8X4),
-                lhsT_scale=w2_mx[g][1][:, N * hf : N * (hf + 1)],
+                lhsT=w2_masked[:, g, hf, :].bitcast(FP8X4),
+                lhsT_scale=w2_scales[(g + hf) % 2][:],
                 rhs=codes.bitcast(FP8X4),
                 rhs_scale=scales,
                 start=start,

@@ -16,9 +16,14 @@ FP8X4 = mybir.dt.float8_e4m3fn_x4
 ACT = mybir.ActivationFunctionType
 
 P = 128
-PASSES = 2
-TILES = 4
-HALF = 64
+PACK = 4
+K_PASS = P * PACK
+PASSES = K // K_PASS
+TILES = H // P
+HALF = P // 2
+CELL_HALF = U // 2
+BLOCKS = CELL_HALF // P
+S_HALF = S // 2
 
 
 def tile_picked_unet_relu_p_kernel(tc, x_words, x_scales, w1, w2, skip, offs, cell, out):
@@ -30,15 +35,15 @@ def tile_picked_unet_relu_p_kernel(tc, x_words, x_scales, w1, w2, skip, offs, ce
         offs_t = sb.tile([P, S // 16], U16, name="offs_t")
         cell_t = sb.tile([P, S // 16], U16, name="cell_t")
         xs = sb.tile([P, T], U8, name="xs", align_bytes=64)
-        xw = [sb.tile([P, T], I32, name=f"xw{z}", align_bytes=64) for z in range(PASSES)]
+        xw = [sb.tile([P, T], I32, name=f"xw{s}", align_bytes=64) for s in range(PASSES)]
         ident = sb.tile([P, P], F32, name="ident", align_bytes=64)
 
         nc.gpsimd.memset(xs[:].bitcast(I32), 0)
         nc.sync.dma_start(offs_t[:], offs)
         nc.sync.dma_start(cell_t[:], cell)
 
-        def load_words(z):
-            nc.sync.dma_start(xw[z][:], x_words[z].rearrange("p n t -> p (n t)").bitcast(I32))
+        def load_words(s):
+            nc.sync.dma_start(xw[s][:], x_words[s].rearrange("p n t -> p (n t)").bitcast(I32))
 
         load_words(0)
         for q in range(4):
@@ -46,27 +51,26 @@ def tile_picked_unet_relu_p_kernel(tc, x_words, x_scales, w1, w2, skip, offs, ce
 
         w1_raw = {}
 
-        def load_w1(c0, c1):
-            for z in range(PASSES):
-                raw = sb.tile([P, 4, c1 - c0], F32, name=f"w1raw{c0}_{z}", tag=f"raw{c0 // P}_{z}", align_bytes=64)
-                nc.sync.dma_start(raw[:], w1[512 * z : 512 * (z + 1), c0:c1].rearrange("(p j) c -> p j c", j=4))
-                for t in range(c0 // P, c1 // P):
-                    w1_raw[t, z] = raw[:, :, t * P - c0 : (t + 1) * P - c0]
+        def load_w1(t):
+            for s in range(PASSES):
+                w1_raw[t, s] = sb.tile([P, PACK, P], F32, name=f"w1raw{t}_{s}", tag=f"raw{t}_{s}", align_bytes=64)
+                rows = w1[K_PASS * s : K_PASS * (s + 1), P * t : P * (t + 1)]
+                nc.sync.dma_start(w1_raw[t, s][:], rows.rearrange("(p j) c -> p j c", j=PACK))
 
-        load_w1(0, 128)
-        load_words(1)
-        load_w1(128, 256)
         skip_t = {}
 
         def load_skip(t):
             skip_t[t] = sb.tile([P, U], F32, name=f"skip{t}", align_bytes=64)
             nc.sync.dma_start(skip_t[t][:], skip[P * t : P * (t + 1), :])
 
-        load_w1(256, 384)
-        load_w1(384, 512)
-        w2_raw = sb.tile([P, 4, N], F32, name="w2raw", align_bytes=64)
-        nc.sync.dma_start(w2_raw[:], w2.rearrange("(p j) n -> p j n", j=4))
-        for t in range(TILES):
+        load_w1(0)
+        load_words(1)
+        for t in range(1, TILES):
+            load_w1(t)
+        load_skip(0)
+        w2_raw = sb.tile([P, PACK, N], F32, name="w2raw", tag="w2raw", align_bytes=64)
+        nc.sync.dma_start(w2_raw[:], w2.rearrange("(p j) n -> p j n", j=PACK))
+        for t in range(1, TILES):
             load_skip(t)
 
         make_identity(nc, ident[:])
@@ -77,142 +81,134 @@ def tile_picked_unet_relu_p_kernel(tc, x_words, x_scales, w1, w2, skip, offs, ce
             window.append(win)
         w2_masked = sb.tile([P, 2, 2, N], I32, name="w2m", align_bytes=64)
         nc.gpsimd.memset(w2_masked[:], 0)
-        w2_scales = [sb.tile([P, N], U8, name=f"w2s{s}", align_bytes=64) for s in range(2)]
+        w2_scales = [sb.tile([P, N], U8, name=f"w2s{swap}", align_bytes=64) for swap in range(2)]
         nc.gpsimd.memset(w2_scales[0][:].bitcast(I32), 0)
 
         w1_codes, w1_scales = {}, {}
 
         def quantise_w1(t):
-            wb = sb.tile([P, PASSES, P, 4], BF16, name=f"w1b{t}", tag=f"w1b{t}", align_bytes=64)
-            for z in range(PASSES):
-                nc.scalar.activation(
-                    out=wb[:, z],
-                    in_=w1_raw[t, z].rearrange("p j c -> p c j"),
-                    func=ACT.Copy,
-                )
+            wb = sb.tile([P, PASSES, P, PACK], BF16, name=f"w1b{t}", tag=f"w1b{t}", align_bytes=64)
+            for s in range(PASSES):
+                nc.scalar.activation(out=wb[:, s], in_=w1_raw[t, s][:].rearrange("p j c -> p c j"), func=ACT.Copy)
             codes = sb.tile([P, PASSES * P], U32, name=f"w1c{t}", align_bytes=64)
             scales = sb.tile([P, PASSES * P], U8, name=f"w1s{t}", align_bytes=64)
-            nc.vector.quantize_mx(out=codes[:].bitcast(FP8X4), scales=scales[:], in_=wb[:].rearrange("p z c j -> p (z c j)"))
+            nc.vector.quantize_mx(out=codes[:].bitcast(FP8X4), scales=scales[:], in_=wb[:].rearrange("p s c j -> p (s c j)"))
             w1_codes[t], w1_scales[t] = codes, scales
 
-        gs = sb.tile([P, S], U8, name="gs", align_bytes=64)
-        gw = {}
+        picked_scales = sb.tile([P, S], U8, name="picked_scales", align_bytes=64)
+        picked_words = {}
 
-        def gather_words(z, j0, j1):
-            nc.vector.tensor_copy(gw[z][:, j0:j1], xw[z][:].bitcast(U32).indirect(offs_t[:, j0 // 16 : j1 // 16]))
+        def gather_words(s, j0, j1):
+            nc.vector.tensor_copy(picked_words[s][:, j0:j1], xw[s][:].bitcast(U32).indirect(offs_t[:, j0 // 16 : j1 // 16]))
 
-        banks = ["acc0", "acc1", "acc2", "acc3"]
+        def relu_on_vector(dst, src):
+            nc.vector.tensor_scalar_max(dst, src, 0.0)
 
-        def first_layer(t, j0, j1, bank, slot):
+        def relu_on_scalar(dst, src):
+            nc.scalar.activation(out=dst, in_=src, func=ACT.Relu)
+
+        def first_layer(t, j0, j1, bank, slot, relu):
             acc = ps.tile([P, j1 - j0], F32, name=f"h{t}_{j0}", tag=bank)
-            for z in range(PASSES):
+            for s in range(PASSES):
                 nc.tensor.matmul_mx(
                     out=acc[:],
-                    lhsT=w1_codes[t][:, P * z : P * (z + 1)].bitcast(FP8X4),
-                    lhsT_scale=w1_scales[t][:, P * z : P * (z + 1)],
-                    rhs=gw[z][:, j0:j1].bitcast(FP8X4),
-                    rhs_scale=gs[4 * z : P, j0:j1],
-                    start=(z == 0),
-                    stop=(z == PASSES - 1),
+                    lhsT=w1_codes[t][:, P * s : P * (s + 1)].bitcast(FP8X4),
+                    lhsT_scale=w1_scales[t][:, P * s : P * (s + 1)],
+                    rhs=picked_words[s][:, j0:j1].bitcast(FP8X4),
+                    rhs_scale=picked_scales[4 * s : P, j0:j1],
+                    start=(s == 0),
+                    stop=(s == PASSES - 1),
                 )
             h = sb.tile([P, j1 - j0], F32, name=f"hs{t}_{j0}", tag=slot, align_bytes=64)
-            if (t, j0) == (0, 0):
-                nc.vector.tensor_scalar_max(h[:], acc[:], 0.0)
-            else:
-                nc.scalar.activation(out=h[:], in_=acc[:], func=ACT.Relu)
+            relu(h[:], acc[:])
             return h
 
         def scatter(t, j0, j1, h):
             nc.vector.tensor_copy(window[t][:].indirect(cell_t[:, j0 // 16 : j1 // 16]), h[:])
 
-        zt = {}
-
-        def turn_and_add(t, groups, copies):
-            g, tl = divmod(t, 2)
-            zbank = []
-            for tag, cs in groups:
+        def turn_and_add(t, banks, empty):
+            sums = []
+            for tag, cs in banks:
                 zb = ps.tile([P, len(cs), 2, P], F32, name=f"zb{t}_{tag}", tag=tag)
-                zbank.append(zb)
-                blocks = [(n, c, hf) for n, c in enumerate(cs) for hf in range(2)]
-                for n, c, hf in blocks:
-                    v0 = 512 * hf + P * c
-                    nc.tensor.matmul(zb[:, n, hf, :], skip_t[t][:, v0 : v0 + P], ident[:], start=(n == 0 and hf == 0), stop=False, is_transpose=True)
-            for zb, (tag, cs) in zip(zbank, groups):
-                blocks = [(n, c, hf) for n, c in enumerate(cs) for hf in range(2)]
-                for n, c, hf in blocks:
-                    v0 = 512 * hf + P * c
-                    nc.tensor.matmul(zb[:, n, hf, :], window[t][:, v0 : v0 + P], ident[:], start=False, stop=(n == len(cs) - 1 and hf == 1), is_transpose=True)
-                if g == 0:
-                    dst = zt_a[cs[0] // 2][:].rearrange("p c (u h t r e) -> p c h u t r e", u=2, h=2, t=2, e=2)[:, :, :, :, tl]
-                    copies[0](dst, zb[:].rearrange("p c h (r u e) -> p c h u r e", u=2, e=2))
-                    continue
+                places = [(zb[:, n, hf, :], CELL_HALF * hf + P * c) for n, c in enumerate(cs) for hf in range(2)]
+                sums.append((zb, cs, places))
+                for m, (dst, v0) in enumerate(places):
+                    nc.tensor.matmul(dst, skip_t[t][:, v0 : v0 + P], ident[:], start=(m == 0), stop=False, is_transpose=True)
+            for zb, cs, places in sums:
+                for m, (dst, v0) in enumerate(places):
+                    nc.tensor.matmul(dst, window[t][:, v0 : v0 + P], ident[:], start=False, stop=(m == len(places) - 1), is_transpose=True)
+                empty(zb, cs)
+
+        def empty_early(t):
+            def empty(zb, cs):
+                dst = turned_early[cs[0] // 2][:].rearrange("p c (u h t r e) -> p c h u t r e", u=2, h=2, t=2, e=2)[:, :, :, :, t % 2]
+                nc.scalar.copy(dst, zb[:].rearrange("p c h (r u e) -> p c h u r e", u=2, e=2))
+
+            return empty
+
+        def empty_late(t, copies):
+            def empty(zb, cs):
                 for n, c in enumerate(cs):
-                    dst = zt[g, c].rearrange("p (u h t r e) -> p u h t r e", u=2, h=2, t=2, e=2)[:, :, :, tl]
+                    dst = turned_late[c][:].rearrange("p (u h t r e) -> p u h t r e", u=2, h=2, t=2, e=2)[:, :, :, t % 2]
                     copies[c](dst, zb[:, n].rearrange("p h (r u e) -> p u h r e", u=2, e=2))
 
-        def turn_back(g, c, tag, copy, grouped):
-            xt = ps.tile([P, 2, P], F32, name=f"xt{g}_{c}", tag=tag)
-            words = zt[g, c].bitcast(F32)
-            for u in range(2):
-                nc.tensor.transpose(xt[:, u, :], words[:, P * u : P * (u + 1)], ident[:])
-            copy(grouped.rearrange("p (y u) -> p y u", u=2), xt[:].rearrange("p u y -> p y u"))
+            return empty
 
         act, dve = nc.scalar.copy, nc.vector.tensor_copy
-        two_banks = [("turn0", (0, 1)), ("turn1", (2, 3))]
-        four_banks = [(banks[c], (c,)) for c in range(4)]
-        nc.vector.tensor_copy(gs[:], xs[:].indirect(offs_t[:]))
-        gw[0] = sb.tile([P, S], U32, name="gw0", align_bytes=64)
+        acc_banks = [f"acc{c}" for c in range(BLOCKS)]
+        turn_banks = [("turn0", (0, 1)), ("turn1", (2, 3))]
+        back_banks = [("back0", (0, 1)), ("back1", (2, 3))]
+        nc.vector.tensor_copy(picked_scales[:], xs[:].indirect(offs_t[:]))
+        picked_words[0] = sb.tile([P, S], U32, name="picked_words0", align_bytes=64)
         gather_words(0, 0, S)
         quantise_w1(0)
-        gw[1] = sb.tile([P, S], U32, name="gw1", tag="w1b0", align_bytes=64)
-        gather_words(1, 0, 256)
-        h0a = first_layer(0, 0, 256, banks[0], "h0a")
-        gather_words(1, 256, S)
-        scatter(0, 0, 256, h0a)
+        picked_words[1] = sb.tile([P, S], U32, name="picked_words1", tag="w1b0", align_bytes=64)
+        gather_words(1, 0, S_HALF)
+        h0a = first_layer(0, 0, S_HALF, acc_banks[0], "h0a", relu_on_vector)
+        gather_words(1, S_HALF, S)
+        scatter(0, 0, S_HALF, h0a)
         quantise_w1(1)
-        h0b = first_layer(0, 256, S, banks[1], "raw1_1")
-        scatter(0, 256, S, h0b)
+        scatter(0, S_HALF, S, first_layer(0, S_HALF, S, acc_banks[1], "raw1_1", relu_on_scalar))
         quantise_w1(2)
-        h1a = first_layer(1, 0, 256, banks[2], "raw2_1")
-        scatter(1, 0, 256, h1a)
+        scatter(1, 0, S_HALF, first_layer(1, 0, S_HALF, acc_banks[2], "raw2_1", relu_on_scalar))
         quantise_w1(3)
-        h1b = first_layer(1, 256, S, banks[3], "raw3_1")
-        scatter(1, 256, S, h1b)
-        w2_b = sb.tile([P, N, 4], BF16, name="w2b", align_bytes=64)
+        scatter(1, S_HALF, S, first_layer(1, S_HALF, S, acc_banks[3], "raw3_1", relu_on_scalar))
+
+        w2_b = sb.tile([P, N, PACK], BF16, name="w2b", align_bytes=64)
         nc.scalar.activation(out=w2_b[:], in_=w2_raw[:].rearrange("p j n -> p n j"), func=ACT.Copy)
-        w2_codes = sb.tile([P, N], U32, name="w2c", align_bytes=64)
+        w2_codes = sb.tile([P, N], U32, name="w2c", tag="raw3_1", align_bytes=64)
         nc.vector.quantize_mx(out=w2_codes[:].bitcast(FP8X4), scales=w2_scales[0][:], in_=w2_b[:].rearrange("p n j -> p (n j)"))
         halves = [slice(0, HALF), slice(HALF, P)]
         for g in range(2):
             for hf in range(2):
                 nc.sync.dma_start(w2_masked[halves[hf], g, hf, :], w2_codes[halves[g], :].bitcast(I32))
             nc.sync.dma_start(w2_scales[1][halves[1 - g], :].bitcast(I32), w2_scales[0][halves[g], :].bitcast(I32))
-        h2 = first_layer(2, 0, S, banks[3], "h2")
-        h3a = first_layer(3, 0, 256, banks[3], "late")
-        zt_a = [sb.tile([P, 2, 512], BF16, name=f"zt_a{k}", tag=f"zt{k}", align_bytes=64) for k in range(2)]
-        for c in range(4):
-            zt_b = sb.tile([P, 512], BF16, name=f"zt_b{c}", align_bytes=64)
-            zt[1, c] = zt_b[:]
-        turn_and_add(0, two_banks, [act] * 4)
-        scatter(2, 0, S, h2)
-        turn_and_add(1, [("back0", (0, 1)), ("back1", (2, 3))], [act] * 4)
-        grouped_a = sb.tile([P, 4, 256], F32, name="grouped_a", align_bytes=64)
-        for k in range(2):
-            xt = ps.tile([P, 2, 2, P], F32, name=f"xt_a{k}", tag=f"back{k}")
-            words = zt_a[k][:].rearrange("p c w -> p (c w)").bitcast(F32)
-            for n in range(4):
-                nc.tensor.transpose(xt[:, n // 2, n % 2, :], words[:, P * n : P * (n + 1)], ident[:])
-            act(grouped_a[:, 2 * k : 2 * k + 2].rearrange("p c (y u) -> p c y u", u=2), xt[:].rearrange("p c u y -> p c y u"))
-        scatter(3, 0, 256, h3a)
 
-        late_codes = sb.tile([P, 512], U32, name="late_codes", align_bytes=64)
-        za_scales = sb.tile([P, 512], U8, name="zas", align_bytes=64)
-        za_codes = late_codes[:, 0:512]
-        nc.vector.quantize_mx(out=za_codes.bitcast(FP8X4), scales=za_scales[:], in_=grouped_a[:].rearrange("p c w -> p (c w)").bitcast(BF16))
-        h3b = first_layer(3, 256, S, banks[2], "zt1")
-        scatter(3, 256, S, h3b)
-        turn_and_add(2, two_banks, [act] * 4)
-        turn_and_add(3, four_banks, [act, dve, act, dve])
+        h2 = first_layer(2, 0, S, acc_banks[3], "w2raw", relu_on_scalar)
+        turned_early = [sb.tile([P, 2, 4 * P], BF16, name=f"turned_early{k}", align_bytes=64) for k in range(2)]
+        turned_late = [sb.tile([P, 4 * P], BF16, name=f"turned_late{c}", align_bytes=64) for c in range(BLOCKS)]
+        turn_and_add(0, turn_banks, empty_early(0))
+        scatter(2, 0, S, h2)
+        turn_and_add(1, back_banks, empty_early(1))
+        h3a = first_layer(3, 0, S_HALF, acc_banks[3], "h3a", relu_on_scalar)
+        grouped_early = sb.tile([P, BLOCKS, 2 * P], F32, name="grouped_early", align_bytes=64)
+        for k in range(2):
+            xt = ps.tile([P, 2, 2, P], F32, name=f"back_early{k}", tag=f"back{k}")
+            words = turned_early[k][:].rearrange("p c w -> p (c w)").bitcast(F32)
+            for m in range(4):
+                nc.tensor.transpose(xt[:, m // 2, m % 2, :], words[:, P * m : P * (m + 1)], ident[:])
+            act(grouped_early[:, 2 * k : 2 * k + 2].rearrange("p c (y u) -> p c y u", u=2), xt[:].rearrange("p c u y -> p c y u"))
+        scatter(3, 0, S_HALF, h3a)
+        early_codes = sb.tile([P, CELL_HALF], U32, name="early_codes", align_bytes=64)
+        early_scales = sb.tile([P, CELL_HALF], U8, name="early_scales", align_bytes=64)
+        nc.vector.quantize_mx(
+            out=early_codes[:].bitcast(FP8X4),
+            scales=early_scales[:],
+            in_=grouped_early[:].rearrange("p c w -> p (c w)").bitcast(BF16),
+        )
+        scatter(3, S_HALF, S, first_layer(3, S_HALF, S, "back1", "h3b", relu_on_scalar))
+        turn_and_add(2, turn_banks, empty_late(2, [act] * BLOCKS))
+        turn_and_add(3, [(acc_banks[c], (c,)) for c in range(BLOCKS)], empty_late(3, [dve, act, dve, act]))
 
         def second_layer(acc, g, hf, codes, scales, start, stop):
             nc.tensor.matmul_mx(
@@ -226,27 +222,32 @@ def tile_picked_unet_relu_p_kernel(tc, x_words, x_scales, w1, w2, skip, offs, ce
             )
 
         out_banks = ["back0", "back1", "turn0", "turn1"]
-        accs = {}
+        out_acc = {}
         for k in range(2):
-            cols = slice(256 * k, 256 * (k + 1))
+            cols = slice(2 * P * k, 2 * P * (k + 1))
             for hf in range(2):
-                accs[k, hf] = ps.tile([P, 256], F32, name=f"o{k}_{hf}", tag=out_banks[2 * k + hf])
-                second_layer(accs[k, hf][:], 0, hf, za_codes[:, cols], za_scales[:, cols], True, False)
-        grouped_b = []
-        for c in range(4):
-            grouped = sb.tile([P, 256], F32, name=f"grouped_b{c}", align_bytes=64)
-            turn_back(1, c, banks[c], dve if c == 1 else act, grouped[:])
-            grouped_b.append(grouped)
+                out_acc[k, hf] = ps.tile([P, 2 * P], F32, name=f"o{k}_{hf}", tag=out_banks[2 * k + hf])
+                second_layer(out_acc[k, hf][:], 0, hf, early_codes[:, cols], early_scales[:, cols], True, False)
+        grouped_late = []
+        for c, copy in enumerate([dve, act, act, act]):
+            grouped = sb.tile([P, 2 * P], F32, name=f"grouped_late{c}", align_bytes=64)
+            xt = ps.tile([P, 2, P], F32, name=f"back_late{c}", tag=acc_banks[c])
+            words = turned_late[c][:].bitcast(F32)
+            for u in range(2):
+                nc.tensor.transpose(xt[:, u, :], words[:, P * u : P * (u + 1)], ident[:])
+            copy(grouped[:].rearrange("p (y u) -> p y u", u=2), xt[:].rearrange("p u y -> p y u"))
+            grouped_late.append(grouped)
+        out_copies = [[act, act], [act, dve]]
         for k in range(2):
-            codes = sb.tile([P, 256], U32, name=f"zc{k}", align_bytes=64)
-            scales = sb.tile([P, 256], U8, name=f"zs{k}", align_bytes=64)
-            for cl in range(2):
-                cols = slice(P * cl, P * (cl + 1))
-                nc.vector.quantize_mx(out=codes[:, cols].bitcast(FP8X4), scales=scales[:, cols], in_=grouped_b[2 * k + cl][:].bitcast(BF16))
+            codes = sb.tile([P, 2 * P], U32, name=f"late_codes{k}", align_bytes=64)
+            scales = sb.tile([P, 2 * P], U8, name=f"late_scales{k}", align_bytes=64)
+            for n in range(2):
+                cols = slice(P * n, P * (n + 1))
+                nc.vector.quantize_mx(out=codes[:, cols].bitcast(FP8X4), scales=scales[:, cols], in_=grouped_late[2 * k + n][:].bitcast(BF16))
                 for hf in range(2):
-                    second_layer(accs[k, hf][:, cols], 1, hf, codes[:, cols], scales[:, cols], False, cl == 1)
+                    second_layer(out_acc[k, hf][:, cols], 1, hf, codes[:, cols], scales[:, cols], False, n == 1)
             for hf in range(2):
-                res = sb.tile([P, 256], F32, name=f"res{k}_{hf}", align_bytes=64)
-                (dve if (k, hf) == (1, 1) else act)(res[:], accs[k, hf][:])
-                v0 = 512 * hf + 256 * k
-                nc.sync.dma_start(out[:, v0 : v0 + 256], res[:])
+                res = sb.tile([P, 2 * P], F32, name=f"res{k}_{hf}", align_bytes=64)
+                out_copies[k][hf](res[:], out_acc[k, hf][:])
+                v0 = CELL_HALF * hf + 2 * P * k
+                nc.sync.dma_start(out[:, v0 : v0 + 2 * P], res[:])

@@ -35,19 +35,18 @@ def tile_picked_unet_relu_p_kernel(tc, x_words, x_scales, w1, w2, skip, offs, ce
         offs_t = sb.tile([P, S // 16], U16, name="offs_t")
         cell_t = sb.tile([P, S // 16], U16, name="cell_t")
         xs = sb.tile([P, T], U8, name="xs", align_bytes=64)
-        xw = [sb.tile([P, T], I32, name=f"xw{s}", align_bytes=64) for s in range(PASSES)]
+        xw = [sb.tile([P, T], I32, name=f"xw{s}", tag=f"xw{s}", align_bytes=64) for s in range(PASSES)]
         ident = sb.tile([P, P], F32, name="ident", align_bytes=64)
 
         nc.gpsimd.memset(xs[:].bitcast(I32), 0)
-        nc.sync.dma_start(offs_t[:], offs)
-        nc.sync.dma_start(cell_t[:], cell)
 
         def load_words(s):
             nc.sync.dma_start(xw[s][:], x_words[s].rearrange("p n t -> p (n t)").bitcast(I32))
 
-        load_words(0)
-        for q in range(4):
-            nc.sync.dma_start(xs[32 * q : 32 * q + 8, :].bitcast(I32), x_scales[:, 4 * q : 4 * q + 4, :].bitcast(I32))
+        def load_scales(s):
+            rows = x_scales[s].rearrange("(q r) n -> r q n", r=4)
+            for r in range(4):
+                nc.sync.dma_start(xs[4 * s + r : P : 32, :].bitcast(I32), rows[r].bitcast(I32))
 
         w1_raw = {}
 
@@ -64,7 +63,11 @@ def tile_picked_unet_relu_p_kernel(tc, x_words, x_scales, w1, w2, skip, offs, ce
             nc.sync.dma_start(skip_t[t][:], skip[P * t : P * (t + 1), :])
 
         load_w1(0)
-        load_words(1)
+        nc.sync.dma_start(offs_t[:], offs)
+        for s in range(PASSES):
+            load_scales(s)
+            load_words(s)
+        nc.sync.dma_start(cell_t[:], cell)
         for t in range(1, TILES):
             load_w1(t)
         load_skip(0)
@@ -95,7 +98,6 @@ def tile_picked_unet_relu_p_kernel(tc, x_words, x_scales, w1, w2, skip, offs, ce
             nc.vector.quantize_mx(out=codes[:].bitcast(FP8X4), scales=scales[:], in_=wb[:].rearrange("p s c j -> p (s c j)"))
             w1_codes[t], w1_scales[t] = codes, scales
 
-        picked_scales = sb.tile([P, S], U8, name="picked_scales", align_bytes=64)
         picked_words = {}
 
         def gather_words(s, j0, j1):
@@ -158,10 +160,11 @@ def tile_picked_unet_relu_p_kernel(tc, x_words, x_scales, w1, w2, skip, offs, ce
         acc_banks = [f"acc{c}" for c in range(BLOCKS)]
         turn_banks = [("turn0", (0, 1)), ("turn1", (2, 3))]
         back_banks = [("back0", (0, 1)), ("back1", (2, 3))]
-        nc.vector.tensor_copy(picked_scales[:], xs[:].indirect(offs_t[:]))
+        quantise_w1(0)
         picked_words[0] = sb.tile([P, S], U32, name="picked_words0", align_bytes=64)
         gather_words(0, 0, S)
-        quantise_w1(0)
+        picked_scales = sb.tile([P, S], U8, name="picked_scales", tag="xw0", align_bytes=64)
+        nc.vector.tensor_copy(picked_scales[:], xs[:].indirect(offs_t[:]))
         picked_words[1] = sb.tile([P, S], U32, name="picked_words1", tag="w1b0", align_bytes=64)
         gather_words(1, 0, S_HALF)
         h0a = first_layer(0, 0, S_HALF, acc_banks[0], "h0a", relu_on_vector)

@@ -68,9 +68,10 @@ def tile_picked_unet_relu_p_kernel(tc, x_words, x_scales, w1, w2, skip, offs, ce
             load_scales(s)
             load_words(s)
         nc.sync.dma_start(cell_t[:], cell)
-        for t in range(1, TILES):
+        for t in range(1, TILES - 1):
             load_w1(t)
         load_skip(0)
+        load_w1(TILES - 1)
         w2_raw = sb.tile([P, PACK, N], F32, name="w2raw", tag="w2raw", align_bytes=64)
         nc.sync.dma_start(w2_raw[:], w2.rearrange("(p j) n -> p j n", j=PACK))
         for t in range(1, TILES):
@@ -128,7 +129,7 @@ def tile_picked_unet_relu_p_kernel(tc, x_words, x_scales, w1, w2, skip, offs, ce
         def scatter(t, j0, j1, h):
             nc.vector.tensor_copy(window[t][:].indirect(cell_t[:, j0 // 16 : j1 // 16]), h[:])
 
-        def turn_and_add(t, banks, empty):
+        def turn_skip(t, banks):
             sums = []
             for tag, cs in banks:
                 zb = ps.tile([P, len(cs), 2, P], F32, name=f"zb{t}_{tag}", tag=tag)
@@ -136,6 +137,9 @@ def tile_picked_unet_relu_p_kernel(tc, x_words, x_scales, w1, w2, skip, offs, ce
                 sums.append((zb, cs, places))
                 for m, (dst, v0) in enumerate(places):
                     nc.tensor.matmul(dst, skip_t[t][:, v0 : v0 + P], ident[:], start=(m == 0), stop=False, is_transpose=True)
+            return sums
+
+        def add_window(t, sums, empty):
             for zb, cs, places in sums:
                 for m, (dst, v0) in enumerate(places):
                     nc.tensor.matmul(dst, window[t][:, v0 : v0 + P], ident[:], start=False, stop=(m == len(places) - 1), is_transpose=True)
@@ -163,7 +167,7 @@ def tile_picked_unet_relu_p_kernel(tc, x_words, x_scales, w1, w2, skip, offs, ce
         quantise_w1(0)
         picked_words[0] = sb.tile([P, S], U32, name="picked_words0", align_bytes=64)
         gather_words(0, 0, S)
-        picked_scales = sb.tile([P, S], U8, name="picked_scales", tag="xw0", align_bytes=64)
+        picked_scales = sb.tile([P, S], U8, name="picked_scales", align_bytes=64)
         nc.vector.tensor_copy(picked_scales[:], xs[:].indirect(offs_t[:]))
         picked_words[1] = sb.tile([P, S], U32, name="picked_words1", tag="w1b0", align_bytes=64)
         gather_words(1, 0, S_HALF)
@@ -179,7 +183,7 @@ def tile_picked_unet_relu_p_kernel(tc, x_words, x_scales, w1, w2, skip, offs, ce
 
         w2_b = sb.tile([P, N, PACK], BF16, name="w2b", align_bytes=64)
         nc.scalar.activation(out=w2_b[:], in_=w2_raw[:].rearrange("p j n -> p n j"), func=ACT.Copy)
-        w2_codes = sb.tile([P, N], U32, name="w2c", tag="raw3_1", align_bytes=64)
+        w2_codes = sb.tile([P, N], U32, name="w2c", align_bytes=64)
         nc.vector.quantize_mx(out=w2_codes[:].bitcast(FP8X4), scales=w2_scales[0][:], in_=w2_b[:].rearrange("p n j -> p (n j)"))
         halves = [slice(0, HALF), slice(HALF, P)]
         for g in range(2):
@@ -190,9 +194,9 @@ def tile_picked_unet_relu_p_kernel(tc, x_words, x_scales, w1, w2, skip, offs, ce
         h2 = first_layer(2, 0, S, acc_banks[3], "w2raw", relu_on_scalar)
         turned_early = [sb.tile([P, 2, 4 * P], BF16, name=f"turned_early{k}", align_bytes=64) for k in range(2)]
         turned_late = [sb.tile([P, 4 * P], BF16, name=f"turned_late{c}", align_bytes=64) for c in range(BLOCKS)]
-        turn_and_add(0, turn_banks, empty_early(0))
+        add_window(0, turn_skip(0, turn_banks), empty_early(0))
         scatter(2, 0, S, h2)
-        turn_and_add(1, back_banks, empty_early(1))
+        add_window(1, turn_skip(1, back_banks), empty_early(1))
         h3a = first_layer(3, 0, S_HALF, acc_banks[3], "h3a", relu_on_scalar)
         grouped_early = sb.tile([P, BLOCKS, 2 * P], F32, name="grouped_early", align_bytes=64)
         for k in range(2):
@@ -209,9 +213,9 @@ def tile_picked_unet_relu_p_kernel(tc, x_words, x_scales, w1, w2, skip, offs, ce
             scales=early_scales[:],
             in_=grouped_early[:].rearrange("p c w -> p (c w)").bitcast(BF16),
         )
-        scatter(3, S_HALF, S, first_layer(3, S_HALF, S, "back1", "h3b", relu_on_scalar))
-        turn_and_add(2, turn_banks, empty_late(2, [act] * BLOCKS))
-        turn_and_add(3, [(acc_banks[c], (c,)) for c in range(BLOCKS)], empty_late(3, [dve, act, dve, act]))
+        scatter(3, S_HALF, S, first_layer(3, S_HALF, S, "back0", "h3b", relu_on_scalar))
+        add_window(2, turn_skip(2, turn_banks), empty_late(2, [act] * BLOCKS))
+        last_sums = turn_skip(3, [(acc_banks[c], (c,)) for c in range(BLOCKS)])
 
         def second_layer(acc, g, hf, codes, scales, start, stop):
             nc.tensor.matmul_mx(
@@ -231,6 +235,7 @@ def tile_picked_unet_relu_p_kernel(tc, x_words, x_scales, w1, w2, skip, offs, ce
             for hf in range(2):
                 out_acc[k, hf] = ps.tile([P, 2 * P], F32, name=f"o{k}_{hf}", tag=out_banks[2 * k + hf])
                 second_layer(out_acc[k, hf][:], 0, hf, early_codes[:, cols], early_scales[:, cols], True, False)
+        add_window(3, last_sums, empty_late(3, [dve, act, dve, act]))
         grouped_late = []
         for c, copy in enumerate([dve, act, act, act]):
             grouped = sb.tile([P, 2 * P], F32, name=f"grouped_late{c}", align_bytes=64)

@@ -1,7 +1,6 @@
 from contextlib import ExitStack
 
 import concourse.mybir as mybir
-from concourse.masks import make_identity
 
 K, T, S, H, N, U = 1024, 2048, 512, 512, 128, 1024
 FLOPS = 2 * K * H * S + 2 * H * N * U
@@ -14,16 +13,15 @@ U16 = mybir.dt.uint16
 U8 = mybir.dt.uint8
 FP8X4 = mybir.dt.float8_e4m3fn_x4
 ACT = mybir.ActivationFunctionType
+ALU = mybir.AluOpType
 
 P = 128
 PACK = 4
 K_PASS = P * PACK
 PASSES = K // K_PASS
-TILES = H // P
-HALF = P // 2
-CELL_HALF = U // 2
-BLOCKS = CELL_HALF // P
 S_HALF = S // 2
+CHUNK = 256
+CHUNKS = U // CHUNK
 
 
 def tile_picked_unet_relu_p_kernel(tc, x_words, x_scales, w1, w2, skip, offs, cell, out):
@@ -35,227 +33,167 @@ def tile_picked_unet_relu_p_kernel(tc, x_words, x_scales, w1, w2, skip, offs, ce
         offs_t = sb.tile([P, S // 16], U16, name="offs_t")
         cell_t = sb.tile([P, S // 16], U16, name="cell_t")
         xs = sb.tile([P, T], U8, name="xs", align_bytes=64)
-        xw = [sb.tile([P, T], I32, name=f"xw{s}", tag=f"xw{s}", align_bytes=64) for s in range(PASSES)]
-        ident = sb.tile([P, P], F32, name="ident", align_bytes=64)
+        xw = [sb.tile([P, T], I32, name=f"xw{s}", align_bytes=64) for s in range(PASSES)]
+        w1_raw = [sb.tile([P, PACK, H], F32, name=f"w1raw{s}", align_bytes=64) for s in range(PASSES)]
+        skip_t = [sb.tile([P, U], F32, name=f"skip{t}", align_bytes=64) for t in range(PACK)]
+        w2_raw = sb.tile([P, PACK, N], F32, name="w2raw", align_bytes=64)
 
         nc.gpsimd.memset(xs[:].bitcast(I32), 0)
 
-        def load_words(s):
-            nc.sync.dma_start(xw[s][:], x_words[s].rearrange("p n t -> p (n t)").bitcast(I32))
-
-        def load_scales(s):
-            rows = x_scales[s].rearrange("(q r) n -> r q n", r=4)
-            for r in range(4):
+        def load_scales(r):
+            for s in range(PASSES):
+                rows = x_scales[s].rearrange("(q r) n -> r q n", r=4)
                 nc.sync.dma_start(xs[4 * s + r : P : 32, :].bitcast(I32), rows[r].bitcast(I32))
 
-        w1_raw = {}
+        def load_pass(s):
+            nc.sync.dma_start(w1_raw[s][:], w1[K_PASS * s : K_PASS * (s + 1), :].rearrange("(p j) c -> p j c", j=PACK))
+            nc.sync.dma_start(xw[s][:], x_words[s].rearrange("p n t -> p (n t)").bitcast(I32))
 
-        def load_w1(t):
-            for s in range(PASSES):
-                w1_raw[t, s] = sb.tile([P, PACK, P], F32, name=f"w1raw{t}_{s}", tag=f"raw{t}_{s}", align_bytes=64)
-                rows = w1[K_PASS * s : K_PASS * (s + 1), P * t : P * (t + 1)]
-                nc.sync.dma_start(w1_raw[t, s][:], rows.rearrange("(p j) c -> p j c", j=PACK))
-
-        skip_t = {}
-
-        def load_skip(t):
-            skip_t[t] = sb.tile([P, U], F32, name=f"skip{t}", align_bytes=64)
-            nc.sync.dma_start(skip_t[t][:], skip[P * t : P * (t + 1), :])
-
-        load_w1(0)
         nc.sync.dma_start(offs_t[:], offs)
-        for s in range(PASSES):
-            load_scales(s)
-            load_words(s)
+        load_scales(0)
+        load_scales(1)
+        load_pass(0)
+        load_scales(2)
+        load_scales(3)
+        load_pass(1)
         nc.sync.dma_start(cell_t[:], cell)
-        for t in range(1, TILES - 1):
-            load_w1(t)
-        load_skip(0)
-        load_w1(TILES - 1)
-        w2_raw = sb.tile([P, PACK, N], F32, name="w2raw", tag="w2raw", align_bytes=64)
-        nc.sync.dma_start(w2_raw[:], w2.rearrange("(p j) n -> p j n", j=PACK))
-        for t in range(1, TILES):
-            load_skip(t)
+        skip_planes = skip.rearrange("(b t r) v -> t b r v", t=PACK, r=8)
+        w2_planes = w2.rearrange("(b t r) n -> t b r n", t=PACK, r=8)
+        for t in range(PACK):
+            nc.sync.dma_start(w2_raw[:, t, :], w2_planes[t])
+        for t in range(PACK):
+            nc.sync.dma_start(skip_t[t][:], skip_planes[t])
 
-        make_identity(nc, ident[:])
         window = []
-        for t in range(TILES):
+        for t in range(PACK):
             win = sb.tile([P, U], F32, name=f"window{t}", align_bytes=64)
             nc.vector.memset(win[:], 0.0)
             window.append(win)
-        w2_masked = sb.tile([P, 2, 2, N], I32, name="w2m", align_bytes=64)
-        nc.gpsimd.memset(w2_masked[:], 0)
-        w2_scales = [sb.tile([P, N], U8, name=f"w2s{swap}", align_bytes=64) for swap in range(2)]
-        nc.gpsimd.memset(w2_scales[0][:].bitcast(I32), 0)
+
+        act, dve = nc.scalar.copy, nc.vector.tensor_copy
 
         w1_codes, w1_scales = {}, {}
 
-        def quantise_w1(t):
-            wb = sb.tile([P, PASSES, P, PACK], BF16, name=f"w1b{t}", tag=f"w1b{t}", align_bytes=64)
-            for s in range(PASSES):
-                nc.scalar.activation(out=wb[:, s], in_=w1_raw[t, s][:].rearrange("p j c -> p c j"), func=ACT.Copy)
-            codes = sb.tile([P, PASSES * P], U32, name=f"w1c{t}", align_bytes=64)
-            scales = sb.tile([P, PASSES * P], U8, name=f"w1s{t}", align_bytes=64)
-            nc.vector.quantize_mx(out=codes[:].bitcast(FP8X4), scales=scales[:], in_=wb[:].rearrange("p s c j -> p (s c j)"))
-            w1_codes[t], w1_scales[t] = codes, scales
+        def quantise_w1(s):
+            src = w1_raw[s][:].rearrange("p j (b a e r) -> p a e b r j", a=2, e=2, r=8)
+            for a, cast in enumerate([dve, act]):
+                wb = sb.tile([P, 2, P, PACK], BF16, name=f"w1b{s}_{a}", align_bytes=64)
+                cast(wb[:].rearrange("p e (b r) j -> p e b r j", r=8), src[:, a])
+                codes = sb.tile([P, 2 * P], U32, name=f"w1c{s}_{a}", align_bytes=64)
+                scales = sb.tile([P, 2 * P], U8, name=f"w1s{s}_{a}", align_bytes=64)
+                nc.vector.quantize_mx(out=codes[:].bitcast(FP8X4), scales=scales[:], in_=wb[:].rearrange("p e m j -> p (e m j)"))
+                for e in range(2):
+                    w1_codes[s, 2 * a + e] = codes[:, P * e : P * (e + 1)]
+                    w1_scales[s, 2 * a + e] = scales[:, P * e : P * (e + 1)]
 
-        picked_words = {}
+        picked_scales = sb.tile([P, S], U8, name="picked_scales", align_bytes=64)
+        picked_words = [sb.tile([P, S], U32, name=f"picked_words{s}", align_bytes=64) for s in range(PASSES)]
 
         def gather_words(s, j0, j1):
             nc.vector.tensor_copy(picked_words[s][:, j0:j1], xw[s][:].bitcast(U32).indirect(offs_t[:, j0 // 16 : j1 // 16]))
 
-        def relu_on_vector(dst, src):
-            nc.vector.tensor_scalar_max(dst, src, 0.0)
-
-        def relu_on_scalar(dst, src):
-            nc.scalar.activation(out=dst, in_=src, func=ACT.Relu)
-
-        def first_layer(t, j0, j1, bank, slot, relu):
-            acc = ps.tile([P, j1 - j0], F32, name=f"h{t}_{j0}", tag=bank)
-            for s in range(PASSES):
-                nc.tensor.matmul_mx(
-                    out=acc[:],
-                    lhsT=w1_codes[t][:, P * s : P * (s + 1)].bitcast(FP8X4),
-                    lhsT_scale=w1_scales[t][:, P * s : P * (s + 1)],
-                    rhs=picked_words[s][:, j0:j1].bitcast(FP8X4),
-                    rhs_scale=picked_scales[4 * s : P, j0:j1],
-                    start=(s == 0),
-                    stop=(s == PASSES - 1),
-                )
-            h = sb.tile([P, j1 - j0], F32, name=f"hs{t}_{j0}", tag=slot, align_bytes=64)
-            relu(h[:], acc[:])
-            return h
-
-        def scatter(t, j0, j1, h):
-            nc.vector.tensor_copy(window[t][:].indirect(cell_t[:, j0 // 16 : j1 // 16]), h[:])
-
-        def turn_skip(t, banks):
-            sums = []
-            for tag, cs in banks:
-                zb = ps.tile([P, len(cs), 2, P], F32, name=f"zb{t}_{tag}", tag=tag)
-                places = [(zb[:, n, hf, :], CELL_HALF * hf + P * c) for n, c in enumerate(cs) for hf in range(2)]
-                sums.append((zb, cs, places))
-                for m, (dst, v0) in enumerate(places):
-                    nc.tensor.matmul(dst, skip_t[t][:, v0 : v0 + P], ident[:], start=(m == 0), stop=False, is_transpose=True)
-            return sums
-
-        def add_window(t, sums, empty):
-            for zb, cs, places in sums:
-                for m, (dst, v0) in enumerate(places):
-                    nc.tensor.matmul(dst, window[t][:, v0 : v0 + P], ident[:], start=False, stop=(m == len(places) - 1), is_transpose=True)
-                empty(zb, cs)
-
-        def empty_early(t):
-            def empty(zb, cs):
-                dst = turned_early[cs[0] // 2][:].rearrange("p c (u h t r e) -> p c h u t r e", u=2, h=2, t=2, e=2)[:, :, :, :, t % 2]
-                nc.scalar.copy(dst, zb[:].rearrange("p c h (r u e) -> p c h u r e", u=2, e=2))
-
-            return empty
-
-        def empty_late(t, copies):
-            def empty(zb, cs):
-                for n, c in enumerate(cs):
-                    dst = turned_late[c][:].rearrange("p (u h t r e) -> p u h t r e", u=2, h=2, t=2, e=2)[:, :, :, t % 2]
-                    copies[c](dst, zb[:, n].rearrange("p h (r u e) -> p u h r e", u=2, e=2))
-
-            return empty
-
-        act, dve = nc.scalar.copy, nc.vector.tensor_copy
-        acc_banks = [f"acc{c}" for c in range(BLOCKS)]
-        turn_banks = [("turn0", (0, 1)), ("turn1", (2, 3))]
-        back_banks = [("back0", (0, 1)), ("back1", (2, 3))]
-        quantise_w1(0)
-        picked_words[0] = sb.tile([P, S], U32, name="picked_words0", align_bytes=64)
-        gather_words(0, 0, S)
-        picked_scales = sb.tile([P, S], U8, name="picked_scales", align_bytes=64)
-        nc.vector.tensor_copy(picked_scales[:], xs[:].indirect(offs_t[:]))
-        picked_words[1] = sb.tile([P, S], U32, name="picked_words1", tag="w1b0", align_bytes=64)
-        gather_words(1, 0, S_HALF)
-        h0a = first_layer(0, 0, S_HALF, acc_banks[0], "h0a", relu_on_vector)
-        gather_words(1, S_HALF, S)
-        scatter(0, 0, S_HALF, h0a)
-        quantise_w1(1)
-        scatter(0, S_HALF, S, first_layer(0, S_HALF, S, acc_banks[1], "raw1_1", relu_on_scalar))
-        quantise_w1(2)
-        scatter(1, 0, S_HALF, first_layer(1, 0, S_HALF, acc_banks[2], "raw2_1", relu_on_scalar))
-        quantise_w1(3)
-        scatter(1, S_HALF, S, first_layer(1, S_HALF, S, acc_banks[3], "raw3_1", relu_on_scalar))
-
-        w2_b = sb.tile([P, N, PACK], BF16, name="w2b", align_bytes=64)
-        nc.scalar.activation(out=w2_b[:], in_=w2_raw[:].rearrange("p j n -> p n j"), func=ACT.Copy)
-        w2_codes = sb.tile([P, N], U32, name="w2c", align_bytes=64)
-        nc.vector.quantize_mx(out=w2_codes[:].bitcast(FP8X4), scales=w2_scales[0][:], in_=w2_b[:].rearrange("p n j -> p (n j)"))
-        halves = [slice(0, HALF), slice(HALF, P)]
-        for g in range(2):
-            for hf in range(2):
-                nc.sync.dma_start(w2_masked[halves[hf], g, hf, :], w2_codes[halves[g], :].bitcast(I32))
-            nc.sync.dma_start(w2_scales[1][halves[1 - g], :].bitcast(I32), w2_scales[0][halves[g], :].bitcast(I32))
-
-        h2 = first_layer(2, 0, S, acc_banks[3], "w2raw", relu_on_scalar)
-        turned_early = [sb.tile([P, 2, 4 * P], BF16, name=f"turned_early{k}", align_bytes=64) for k in range(2)]
-        turned_late = [sb.tile([P, 4 * P], BF16, name=f"turned_late{c}", align_bytes=64) for c in range(BLOCKS)]
-        add_window(0, turn_skip(0, turn_banks), empty_early(0))
-        scatter(2, 0, S, h2)
-        add_window(1, turn_skip(1, back_banks), empty_early(1))
-        h3a = first_layer(3, 0, S_HALF, acc_banks[3], "h3a", relu_on_scalar)
-        grouped_early = sb.tile([P, BLOCKS, 2 * P], F32, name="grouped_early", align_bytes=64)
-        for k in range(2):
-            xt = ps.tile([P, 2, 2, P], F32, name=f"back_early{k}", tag=f"back{k}")
-            words = turned_early[k][:].rearrange("p c w -> p (c w)").bitcast(F32)
-            for m in range(4):
-                nc.tensor.transpose(xt[:, m // 2, m % 2, :], words[:, P * m : P * (m + 1)], ident[:])
-            act(grouped_early[:, 2 * k : 2 * k + 2].rearrange("p c (y u) -> p c y u", u=2), xt[:].rearrange("p c u y -> p c y u"))
-        scatter(3, 0, S_HALF, h3a)
-        early_codes = sb.tile([P, CELL_HALF], U32, name="early_codes", align_bytes=64)
-        early_scales = sb.tile([P, CELL_HALF], U8, name="early_scales", align_bytes=64)
-        nc.vector.quantize_mx(
-            out=early_codes[:].bitcast(FP8X4),
-            scales=early_scales[:],
-            in_=grouped_early[:].rearrange("p c w -> p (c w)").bitcast(BF16),
-        )
-        scatter(3, S_HALF, S, first_layer(3, S_HALF, S, "back0", "h3b", relu_on_scalar))
-        add_window(2, turn_skip(2, turn_banks), empty_late(2, [act] * BLOCKS))
-        last_sums = turn_skip(3, [(acc_banks[c], (c,)) for c in range(BLOCKS)])
-
-        def second_layer(acc, g, hf, codes, scales, start, stop):
+        def first_pass(acc, t, s, j0, j1):
             nc.tensor.matmul_mx(
-                out=acc,
-                lhsT=w2_masked[:, g, hf, :].bitcast(FP8X4),
-                lhsT_scale=w2_scales[(g + hf) % 2][:],
-                rhs=codes.bitcast(FP8X4),
-                rhs_scale=scales,
-                start=start,
-                stop=stop,
+                out=acc[:],
+                lhsT=w1_codes[s, t].bitcast(FP8X4),
+                lhsT_scale=w1_scales[s, t],
+                rhs=picked_words[s][:, j0:j1].bitcast(FP8X4),
+                rhs_scale=picked_scales[4 * s : P, j0:j1],
+                start=(s == 0),
+                stop=(s == PASSES - 1),
             )
 
-        out_banks = ["back0", "back1", "turn0", "turn1"]
-        out_acc = {}
-        for k in range(2):
-            cols = slice(2 * P * k, 2 * P * (k + 1))
-            for hf in range(2):
-                out_acc[k, hf] = ps.tile([P, 2 * P], F32, name=f"o{k}_{hf}", tag=out_banks[2 * k + hf])
-                second_layer(out_acc[k, hf][:], 0, hf, early_codes[:, cols], early_scales[:, cols], True, False)
-        add_window(3, last_sums, empty_late(3, [dve, act, dve, act]))
-        grouped_late = []
-        for c, copy in enumerate([dve, act, act, act]):
-            grouped = sb.tile([P, 2 * P], F32, name=f"grouped_late{c}", align_bytes=64)
-            xt = ps.tile([P, 2, P], F32, name=f"back_late{c}", tag=acc_banks[c])
-            words = turned_late[c][:].bitcast(F32)
-            for u in range(2):
-                nc.tensor.transpose(xt[:, u, :], words[:, P * u : P * (u + 1)], ident[:])
-            copy(grouped[:].rearrange("p (y u) -> p y u", u=2), xt[:].rearrange("p u y -> p y u"))
-            grouped_late.append(grouped)
-        out_copies = [[act, act], [act, dve]]
-        for k in range(2):
-            codes = sb.tile([P, 2 * P], U32, name=f"late_codes{k}", align_bytes=64)
-            scales = sb.tile([P, 2 * P], U8, name=f"late_scales{k}", align_bytes=64)
-            for n in range(2):
-                cols = slice(P * n, P * (n + 1))
-                nc.vector.quantize_mx(out=codes[:, cols].bitcast(FP8X4), scales=scales[:, cols], in_=grouped_late[2 * k + n][:].bitcast(BF16))
-                for hf in range(2):
-                    second_layer(out_acc[k, hf][:, cols], 1, hf, codes[:, cols], scales[:, cols], False, n == 1)
-            for hf in range(2):
-                res = sb.tile([P, 2 * P], F32, name=f"res{k}_{hf}", align_bytes=64)
-                out_copies[k][hf](res[:], out_acc[k, hf][:])
-                v0 = CELL_HALF * hf + 2 * P * k
-                nc.sync.dma_start(out[:, v0 : v0 + 2 * P], res[:])
+        pieces = [(0, 0, S_HALF), (1, 0, S_HALF), (0, S_HALF, S), (1, S_HALF, S), (2, 0, S), (3, 0, S)]
+        accs = {}
+        quantise_w1(0)
+        gather_words(0, 0, S)
+        nc.vector.tensor_copy(picked_scales[:], xs[:].indirect(offs_t[:]))
+        for n, (t, j0, j1) in enumerate(pieces):
+            accs[t, j0] = ps.tile([P, j1 - j0], F32, name=f"h{t}_{j0}", tag=f"bank{n}")
+            first_pass(accs[t, j0], t, 0, j0, j1)
+        quantise_w1(1)
+        gather_words(1, 0, S_HALF)
+        gather_words(1, S_HALF, S)
+        for t, j0, j1 in pieces:
+            first_pass(accs[t, j0], t, 1, j0, j1)
+
+        hs = {}
+
+        def relu(t, j0, j1):
+            hs[t, j0] = sb.tile([P, j1 - j0], F32, name=f"hs{t}_{j0}", align_bytes=64)
+            nc.scalar.activation(out=hs[t, j0][:], in_=accs[t, j0][:], func=ACT.Relu)
+
+        def scatter(t, j0, j1, src):
+            dst = window[t][:].indirect(cell_t[:, j0 // 16 : j1 // 16])
+            if t % 2 == 0:
+                nc.vector.tensor_copy(dst, src)
+            else:
+                nc.scalar.activation(out=dst, in_=src, func=ACT.Copy)
+
+        for piece in pieces[:3]:
+            relu(*piece)
+        scatter(0, 0, S_HALF, hs[0, 0][:])
+        scatter(1, 0, S_HALF, hs[1, 0][:])
+        w2_b = sb.tile([P, N, PACK], BF16, name="w2b", align_bytes=64)
+        dve(w2_b[:], w2_raw[:].rearrange("p j n -> p n j"))
+        scatter(0, S_HALF, S, hs[0, S_HALF][:])
+        w2_codes = sb.tile([P, N], U32, name="w2c", align_bytes=64)
+        w2_scales = sb.tile([P, N], U8, name="w2s", align_bytes=64)
+        nc.vector.quantize_mx(out=w2_codes[:].bitcast(FP8X4), scales=w2_scales[:], in_=w2_b[:].rearrange("p n j -> p (n j)"))
+        for piece in pieces[3:5]:
+            relu(*piece)
+        scatter(1, S_HALF, S, hs[1, S_HALF][:])
+        relu(3, 0, S)
+        scatter(2, 0, S, hs[2, 0][:])
+        scatter(3, 0, S_HALF, hs[3, 0][:, 0:S_HALF])
+        scatter(3, S_HALF, S, hs[3, 0][:, S_HALF:S])
+
+        zb = sb.tile([P, PACK, U], BF16, name="zb", align_bytes=64)
+        for t in range(2):
+            nc.gpsimd.tensor_tensor(zb[:, t, :], window[t][:], skip_t[t][:], ALU.add)
+
+        nc.vector.tensor_tensor(zb[:, 2, :], window[2][:], skip_t[2][:], ALU.add)
+        chunk_cols = [slice(CHUNK * c, CHUNK * (c + 1)) for c in range(CHUNKS)]
+        grouped, accs_out = {}, {}
+
+        def add_last(c):
+            nc.vector.tensor_tensor(zb[:, 3, chunk_cols[c]], window[3][:, chunk_cols[c]], skip_t[3][:, chunk_cols[c]], ALU.add)
+
+        def weave(c, copy):
+            grouped[c] = sb.tile([P, CHUNK, PACK], BF16, name=f"grouped{c}", align_bytes=64)
+            copy(grouped[c][:], zb[:, :, chunk_cols[c]].rearrange("p t v -> p v t"))
+
+        def second_layer(c):
+            codes = sb.tile([P, CHUNK], U32, name=f"zc{c}", align_bytes=64)
+            scales = sb.tile([P, CHUNK], U8, name=f"zs{c}", align_bytes=64)
+            nc.vector.quantize_mx(out=codes[:].bitcast(FP8X4), scales=scales[:], in_=grouped[c][:].rearrange("p v t -> p (v t)"))
+            accs_out[c] = ps.tile([P, CHUNK], F32, name=f"o{c}", tag=f"bank{c}")
+            nc.tensor.matmul_mx(
+                out=accs_out[c][:],
+                lhsT=w2_codes[:].bitcast(FP8X4),
+                lhsT_scale=w2_scales[:],
+                rhs=codes[:].bitcast(FP8X4),
+                rhs_scale=scales[:],
+                start=True,
+                stop=True,
+            )
+
+        def store(c, copy):
+            res = sb.tile([P, CHUNK], F32, name=f"res{c}", align_bytes=64)
+            copy(res[:], accs_out[c][:])
+            nc.sync.dma_start(out[:, chunk_cols[c]], res[:])
+
+        for c in range(CHUNKS):
+            add_last(c)
+        weave(0, act)
+        weave(1, act)
+        weave(2, dve)
+        second_layer(0)
+        weave(3, dve)
+        second_layer(2)
+        second_layer(1)
+        second_layer(3)
+        store(0, act)
+        store(2, act)
+        store(1, act)
+        store(3, dve)

@@ -93,17 +93,19 @@ def tile_picked_unet_relu_p_kernel(tc, x_words, x_scales, w1, w2, skip, offs, ce
             nc.vector.tensor_copy(picked_words[s][:, j0:j1], xw[s][:].bitcast(U32).indirect(offs_t[:, j0 // 16 : j1 // 16]))
 
         def first_pass(acc, t, s, j0, j1):
-            nc.tensor.matmul_mx(
-                out=acc[:],
-                lhsT=w1_codes[s, t].bitcast(FP8X4),
-                lhsT_scale=w1_scales[s, t],
-                rhs=picked_words[s][:, j0:j1].bitcast(FP8X4),
-                rhs_scale=picked_scales[4 * s : P, j0:j1],
-                start=(s == 0),
-                stop=(s == PASSES - 1),
-            )
+            runs = [(j0, j1)] if j1 - j0 != 3 * P else [(j0, j0 + P), (j0 + P, j1)]
+            for n, (c0, c1) in enumerate(runs):
+                nc.tensor.matmul_mx(
+                    out=acc[:, c0 - j0 : c1 - j0],
+                    lhsT=w1_codes[s, t].bitcast(FP8X4),
+                    lhsT_scale=w1_scales[s, t],
+                    rhs=picked_words[s][:, c0:c1].bitcast(FP8X4),
+                    rhs_scale=picked_scales[4 * s : P, c0:c1],
+                    start=(s == 0 and n == 0),
+                    stop=(s == PASSES - 1 and n == len(runs) - 1),
+                )
 
-        pieces = [(0, 0, S_HALF), (1, 0, S_HALF), (0, S_HALF, S), (1, S_HALF, S), (2, 0, S), (3, 0, S)]
+        pieces = [(0, 0, P), (1, 0, P), (0, P, S), (1, P, S), (2, 0, S_HALF), (3, 0, S), (2, S_HALF, S)]
         accs = {}
         quantise_w1(0)
         gather_words(0, 0, S)
@@ -112,56 +114,66 @@ def tile_picked_unet_relu_p_kernel(tc, x_words, x_scales, w1, w2, skip, offs, ce
             accs[t, j0] = ps.tile([P, j1 - j0], F32, name=f"h{t}_{j0}", tag=f"bank{n}")
             first_pass(accs[t, j0], t, 0, j0, j1)
         quantise_w1(1)
-        gather_words(1, 0, S_HALF)
-        gather_words(1, S_HALF, S)
+        gather_words(1, 0, P)
+        gather_words(1, P, S)
         for t, j0, j1 in pieces:
             first_pass(accs[t, j0], t, 1, j0, j1)
 
         hs = {}
 
-        def relu(t, j0, j1):
+        def relu(t, j0, j1, on_vector=False):
             hs[t, j0] = sb.tile([P, j1 - j0], F32, name=f"hs{t}_{j0}", align_bytes=64)
-            nc.scalar.activation(out=hs[t, j0][:], in_=accs[t, j0][:], func=ACT.Relu)
-
-        def scatter(t, j0, j1, src):
-            dst = window[t][:].indirect(cell_t[:, j0 // 16 : j1 // 16])
-            if t % 2 == 0:
-                nc.vector.tensor_copy(dst, src)
+            if on_vector:
+                nc.vector.tensor_scalar_max(hs[t, j0][:], accs[t, j0][:], 0.0)
             else:
-                nc.scalar.activation(out=dst, in_=src, func=ACT.Copy)
+                nc.scalar.activation(out=hs[t, j0][:], in_=accs[t, j0][:], func=ACT.Relu)
 
-        for piece in pieces[:3]:
-            relu(*piece)
-        scatter(0, 0, S_HALF, hs[0, 0][:])
-        scatter(1, 0, S_HALF, hs[1, 0][:])
+        def scatter_v(t, j0, j1, src):
+            nc.vector.tensor_copy(window[t][:].indirect(cell_t[:, j0 // 16 : j1 // 16]), src)
+
+        def scatter_s(t, j0, j1, src):
+            nc.scalar.activation(out=window[t][:].indirect(cell_t[:, j0 // 16 : j1 // 16]), in_=src, func=ACT.Copy)
+
+        zb = sb.tile([P, PACK, U], BF16, name="zb", align_bytes=64)
+
+        def add_plane(t):
+            nc.vector.tensor_tensor(zb[:, t, :], window[t][:], skip_t[t][:], ALU.add)
+
+        relu(0, 0, P)
+        relu(1, 0, P)
+        scatter_v(0, 0, P, hs[0, 0][:])
+        scatter_s(1, 0, P, hs[1, 0][:])
+        relu(0, P, S, True)
         w2_b = sb.tile([P, N, PACK], BF16, name="w2b", align_bytes=64)
         dve(w2_b[:], w2_raw[:].rearrange("p j n -> p n j"))
-        scatter(0, S_HALF, S, hs[0, S_HALF][:])
+        scatter_v(0, P, S, hs[0, P][:])
         w2_codes = sb.tile([P, N], U32, name="w2c", align_bytes=64)
         w2_scales = sb.tile([P, N], U8, name="w2s", align_bytes=64)
         nc.vector.quantize_mx(out=w2_codes[:].bitcast(FP8X4), scales=w2_scales[:], in_=w2_b[:].rearrange("p n j -> p (n j)"))
-        for piece in pieces[3:5]:
-            relu(*piece)
-        scatter(1, S_HALF, S, hs[1, S_HALF][:])
+        relu(1, P, S)
+        relu(2, 0, S_HALF, True)
+        scatter_s(1, P, S, hs[1, P][:])
+        scatter_v(2, 0, S_HALF, hs[2, 0][:])
         relu(3, 0, S)
-        scatter(2, 0, S, hs[2, 0][:])
-        scatter(3, 0, S_HALF, hs[3, 0][:, 0:S_HALF])
-        scatter(3, S_HALF, S, hs[3, 0][:, S_HALF:S])
-
-        zb = sb.tile([P, PACK, U], BF16, name="zb", align_bytes=64)
-        for t in range(2):
-            nc.gpsimd.tensor_tensor(zb[:, t, :], window[t][:], skip_t[t][:], ALU.add)
-
-        nc.vector.tensor_tensor(zb[:, 2, :], window[2][:], skip_t[2][:], ALU.add)
+        relu(2, S_HALF, S)
+        add_plane(0)
+        add_plane(1)
+        scatter_s(3, 0, S_HALF, hs[3, 0][:, 0:S_HALF])
+        scatter_s(2, S_HALF, S, hs[2, S_HALF][:])
+        scatter_s(3, S_HALF, S, hs[3, 0][:, S_HALF:S])
+        add_plane(2)
         chunk_cols = [slice(CHUNK * c, CHUNK * (c + 1)) for c in range(CHUNKS)]
         grouped, accs_out = {}, {}
 
         def add_last(c):
             nc.vector.tensor_tensor(zb[:, 3, chunk_cols[c]], window[3][:, chunk_cols[c]], skip_t[3][:, chunk_cols[c]], ALU.add)
 
-        def weave(c, copy):
+        def weave(c, *copies):
             grouped[c] = sb.tile([P, CHUNK, PACK], BF16, name=f"grouped{c}", align_bytes=64)
-            copy(grouped[c][:], zb[:, :, chunk_cols[c]].rearrange("p t v -> p v t"))
+            width = CHUNK // len(copies)
+            for n, copy in enumerate(copies):
+                v0 = CHUNK * c + width * n
+                copy(grouped[c][:, width * n : width * (n + 1)], zb[:, :, v0 : v0 + width].rearrange("p t v -> p v t"))
 
         def second_layer(c):
             codes = sb.tile([P, CHUNK], U32, name=f"zc{c}", align_bytes=64)
@@ -189,7 +201,7 @@ def tile_picked_unet_relu_p_kernel(tc, x_words, x_scales, w1, w2, skip, offs, ce
         weave(1, act)
         weave(2, dve)
         second_layer(0)
-        weave(3, dve)
+        weave(3, dve, act)
         second_layer(2)
         second_layer(1)
         second_layer(3)

@@ -20,8 +20,7 @@ PACK = 4
 K_PASS = P * PACK
 PASSES = K // K_PASS
 S_HALF = S // 2
-CHUNK = 256
-CHUNKS = U // CHUNK
+SHARE = 224
 
 
 def tile_picked_unet_relu_p_kernel(tc, x_words, x_scales, w1, w2, skip, offs, cell, out):
@@ -32,37 +31,41 @@ def tile_picked_unet_relu_p_kernel(tc, x_words, x_scales, w1, w2, skip, offs, ce
 
         offs_t = sb.tile([P, S // 16], U16, name="offs_t")
         cell_t = sb.tile([P, S // 16], U16, name="cell_t")
-        xs = sb.tile([P, T], U8, name="xs", align_bytes=64)
-        xw = [sb.tile([P, T], I32, name=f"xw{s}", align_bytes=64) for s in range(PASSES)]
-        w1_raw = [sb.tile([P, PACK, H], F32, name=f"w1raw{s}", align_bytes=64) for s in range(PASSES)]
-        skip_t = [sb.tile([P, U], F32, name=f"skip{t}", align_bytes=64) for t in range(PACK)]
-        w2_raw = sb.tile([P, PACK, N], F32, name="w2raw", align_bytes=64)
+        xs = sb.tile([P, T], U8, name="xs", tag="x_late", align_bytes=64)
+        w1_raw = [sb.tile([P, PACK, H], F32, name=f"w1raw{s}", tag=f"w1raw{s}", align_bytes=64) for s in range(PASSES)]
+        xw = [sb.tile([P, T], I32, name="xw0", tag="xw0", align_bytes=64)]
+        planes = [sb.tile([P, S], U8, name=f"plane{s}", align_bytes=64) for s in range(PASSES)]
+        picked_scales = sb.tile([P, S], U8, name="picked_scales", align_bytes=64)
 
-        nc.gpsimd.memset(xs[:].bitcast(I32), 0)
+        nc.gpsimd.memset(xs[32:64, :].bitcast(I32), 0)
+        nc.gpsimd.memset(xs[64:128, :].bitcast(I32), 0)
+        for s in range(PASSES):
+            nc.gpsimd.memset(planes[s][:].bitcast(I32), 0)
 
-        def load_scales(r):
-            for s in range(PASSES):
-                rows = x_scales[s].rearrange("(q r) n -> r q n", r=4)
-                nc.sync.dma_start(xs[4 * s + r : P : 32, :].bitcast(I32), rows[r].bitcast(I32))
-
-        def load_pass(s):
+        def load_w1(s):
             nc.sync.dma_start(w1_raw[s][:], w1[K_PASS * s : K_PASS * (s + 1), :].rearrange("(p j) c -> p j c", j=PACK))
+
+        def load_words(s):
             nc.sync.dma_start(xw[s][:], x_words[s].rearrange("p n t -> p (n t)").bitcast(I32))
 
+        def place_scales(s, q):
+            row = 16 * s + 4 * q
+            nc.sync.dma_start(planes[s][32 * q + 4 * s : 32 * q + 4 * s + 4, :].bitcast(I32), picked_scales[row : row + 4, :].bitcast(I32))
+
+        nc.sync.dma_start(xs[0:32, :].bitcast(I32), x_scales.rearrange("s q n -> (s q) n").bitcast(I32))
         nc.sync.dma_start(offs_t[:], offs)
-        load_scales(0)
-        load_scales(1)
-        load_pass(0)
-        load_scales(2)
-        load_scales(3)
-        load_pass(1)
         nc.sync.dma_start(cell_t[:], cell)
-        skip_planes = skip.rearrange("(b t r) v -> t b r v", t=PACK, r=8)
-        w2_planes = w2.rearrange("(b t r) n -> t b r n", t=PACK, r=8)
-        for t in range(PACK):
-            nc.sync.dma_start(w2_raw[:, t, :], w2_planes[t])
-        for t in range(PACK):
-            nc.sync.dma_start(skip_t[t][:], skip_planes[t])
+        load_w1(0)
+        load_words(0)
+        load_w1(1)
+        nc.vector.tensor_copy(picked_scales[:], xs[:].indirect(offs_t[:]))
+        for q in range(4):
+            place_scales(0, q)
+        place_scales(1, 0)
+        xw.append(sb.tile([P, T], I32, name="xw1", tag="x_late", align_bytes=64))
+        load_words(1)
+        for q in range(1, 4):
+            place_scales(1, q)
 
         window = []
         for t in range(PACK):
@@ -77,7 +80,7 @@ def tile_picked_unet_relu_p_kernel(tc, x_words, x_scales, w1, w2, skip, offs, ce
         def quantise_w1(s):
             src = w1_raw[s][:].rearrange("p j (b a e r) -> p a e b r j", a=2, e=2, r=8)
             for a, cast in enumerate([dve, act]):
-                wb = sb.tile([P, 2, P, PACK], BF16, name=f"w1b{s}_{a}", align_bytes=64)
+                wb = sb.tile([P, 2, P, PACK], BF16, name=f"w1b{s}_{a}", tag=f"w1b{s}_{a}", align_bytes=64)
                 cast(wb[:].rearrange("p e (b r) j -> p e b r j", r=8), src[:, a])
                 codes = sb.tile([P, 2 * P], U32, name=f"w1c{s}_{a}", align_bytes=64)
                 scales = sb.tile([P, 2 * P], U8, name=f"w1s{s}_{a}", align_bytes=64)
@@ -86,7 +89,6 @@ def tile_picked_unet_relu_p_kernel(tc, x_words, x_scales, w1, w2, skip, offs, ce
                     w1_codes[s, 2 * a + e] = codes[:, P * e : P * (e + 1)]
                     w1_scales[s, 2 * a + e] = scales[:, P * e : P * (e + 1)]
 
-        picked_scales = sb.tile([P, S], U8, name="picked_scales", align_bytes=64)
         picked_words = [sb.tile([P, S], U32, name=f"picked_words{s}", align_bytes=64) for s in range(PASSES)]
 
         def gather_words(s, j0, j1):
@@ -100,16 +102,15 @@ def tile_picked_unet_relu_p_kernel(tc, x_words, x_scales, w1, w2, skip, offs, ce
                     lhsT=w1_codes[s, t].bitcast(FP8X4),
                     lhsT_scale=w1_scales[s, t],
                     rhs=picked_words[s][:, c0:c1].bitcast(FP8X4),
-                    rhs_scale=picked_scales[4 * s : P, c0:c1],
+                    rhs_scale=planes[s][4 * s : P, c0:c1],
                     start=(s == 0 and n == 0),
                     stop=(s == PASSES - 1 and n == len(runs) - 1),
                 )
 
-        pieces = [(0, 0, P), (1, 0, P), (0, P, S), (1, P, S), (2, 0, S_HALF), (3, 0, S), (2, S_HALF, S)]
+        pieces = [(1, 0, P), (0, 0, P), (0, P, S), (1, P, S), (2, 0, S), (3, 0, S)]
         accs = {}
         quantise_w1(0)
         gather_words(0, 0, S)
-        nc.vector.tensor_copy(picked_scales[:], xs[:].indirect(offs_t[:]))
         for n, (t, j0, j1) in enumerate(pieces):
             accs[t, j0] = ps.tile([P, j1 - j0], F32, name=f"h{t}_{j0}", tag=f"bank{n}")
             first_pass(accs[t, j0], t, 0, j0, j1)
@@ -118,6 +119,16 @@ def tile_picked_unet_relu_p_kernel(tc, x_words, x_scales, w1, w2, skip, offs, ce
         gather_words(1, P, S)
         for t, j0, j1 in pieces:
             first_pass(accs[t, j0], t, 1, j0, j1)
+
+        skip_planes = skip.rearrange("(b t r) v -> t b r v", t=PACK, r=8)
+        w2_planes = w2.rearrange("(b t r) n -> t b r n", t=PACK, r=8)
+        w2_raw = sb.tile([P, PACK, N], F32, name="w2raw", tag="w1b0_0", align_bytes=64)
+        for t in range(PACK):
+            nc.sync.dma_start(w2_raw[:, t, :], w2_planes[t])
+        skip_t = []
+        for t, slot in enumerate(["w1raw0", "xw0", "w1raw1", "x_late"]):
+            skip_t.append(sb.tile([P, U], F32, name=f"skip{t}", tag=slot, align_bytes=64))
+            nc.sync.dma_start(skip_t[t][:], skip_planes[t])
 
         hs = {}
 
@@ -139,8 +150,8 @@ def tile_picked_unet_relu_p_kernel(tc, x_words, x_scales, w1, w2, skip, offs, ce
         def add_plane(t):
             nc.vector.tensor_tensor(zb[:, t, :], window[t][:], skip_t[t][:], ALU.add)
 
-        relu(0, 0, P)
         relu(1, 0, P)
+        relu(0, 0, P)
         scatter_v(0, 0, P, hs[0, 0][:])
         scatter_s(1, 0, P, hs[1, 0][:])
         relu(0, P, S, True)
@@ -151,35 +162,34 @@ def tile_picked_unet_relu_p_kernel(tc, x_words, x_scales, w1, w2, skip, offs, ce
         w2_scales = sb.tile([P, N], U8, name="w2s", align_bytes=64)
         nc.vector.quantize_mx(out=w2_codes[:].bitcast(FP8X4), scales=w2_scales[:], in_=w2_b[:].rearrange("p n j -> p (n j)"))
         relu(1, P, S)
-        relu(2, 0, S_HALF, True)
-        scatter_s(1, P, S, hs[1, P][:])
-        scatter_v(2, 0, S_HALF, hs[2, 0][:])
+        relu(2, 0, S)
         relu(3, 0, S)
-        relu(2, S_HALF, S)
+        scatter_s(1, P, S, hs[1, P][:])
+        scatter_v(2, SHARE, S, hs[2, 0][:, SHARE:S])
         add_plane(0)
         add_plane(1)
         scatter_s(3, 0, S_HALF, hs[3, 0][:, 0:S_HALF])
-        scatter_s(2, S_HALF, S, hs[2, S_HALF][:])
+        scatter_s(2, 0, SHARE, hs[2, 0][:, 0:SHARE])
         scatter_s(3, S_HALF, S, hs[3, 0][:, S_HALF:S])
         add_plane(2)
-        chunk_cols = [slice(CHUNK * c, CHUNK * (c + 1)) for c in range(CHUNKS)]
+        edges = [0, 256, 512, 768, 896, 1024]
+        chunk_cols = [slice(v0, v1) for v0, v1 in zip(edges, edges[1:])]
         grouped, accs_out = {}, {}
 
-        def add_last(c):
-            nc.vector.tensor_tensor(zb[:, 3, chunk_cols[c]], window[3][:, chunk_cols[c]], skip_t[3][:, chunk_cols[c]], ALU.add)
+        def add_last(c0, c1):
+            cols = slice(edges[c0], edges[c1])
+            nc.vector.tensor_tensor(zb[:, 3, cols], window[3][:, cols], skip_t[3][:, cols], ALU.add)
 
-        def weave(c, *copies):
-            grouped[c] = sb.tile([P, CHUNK, PACK], BF16, name=f"grouped{c}", align_bytes=64)
-            width = CHUNK // len(copies)
-            for n, copy in enumerate(copies):
-                v0 = CHUNK * c + width * n
-                copy(grouped[c][:, width * n : width * (n + 1)], zb[:, :, v0 : v0 + width].rearrange("p t v -> p v t"))
+        def weave(c, copy):
+            grouped[c] = sb.tile([P, edges[c + 1] - edges[c], PACK], BF16, name=f"grouped{c}", align_bytes=64)
+            copy(grouped[c][:], zb[:, :, chunk_cols[c]].rearrange("p t v -> p v t"))
 
         def second_layer(c):
-            codes = sb.tile([P, CHUNK], U32, name=f"zc{c}", align_bytes=64)
-            scales = sb.tile([P, CHUNK], U8, name=f"zs{c}", align_bytes=64)
+            width = edges[c + 1] - edges[c]
+            codes = sb.tile([P, width], U32, name=f"zc{c}", align_bytes=64)
+            scales = sb.tile([P, width], U8, name=f"zs{c}", align_bytes=64)
             nc.vector.quantize_mx(out=codes[:].bitcast(FP8X4), scales=scales[:], in_=grouped[c][:].rearrange("p v t -> p (v t)"))
-            accs_out[c] = ps.tile([P, CHUNK], F32, name=f"o{c}", tag=f"bank{c}")
+            accs_out[c] = ps.tile([P, width], F32, name=f"o{c}", tag=f"bank{c}")
             nc.tensor.matmul_mx(
                 out=accs_out[c][:],
                 lhsT=w2_codes[:].bitcast(FP8X4),
@@ -191,21 +201,20 @@ def tile_picked_unet_relu_p_kernel(tc, x_words, x_scales, w1, w2, skip, offs, ce
             )
 
         def store(c, copy):
-            res = sb.tile([P, CHUNK], F32, name=f"res{c}", align_bytes=64)
+            res = sb.tile([P, edges[c + 1] - edges[c]], F32, name=f"res{c}", align_bytes=64)
             copy(res[:], accs_out[c][:])
             nc.sync.dma_start(out[:, chunk_cols[c]], res[:])
 
-        for c in range(CHUNKS):
-            add_last(c)
+        add_last(0, 1)
+        add_last(1, 2)
+        add_last(2, 5)
         weave(0, act)
-        weave(1, act)
-        weave(2, dve)
+        weave(1, dve)
+        weave(2, act)
         second_layer(0)
-        weave(3, dve, act)
-        second_layer(2)
-        second_layer(1)
-        second_layer(3)
-        store(0, act)
-        store(2, act)
-        store(1, act)
-        store(3, dve)
+        weave(3, dve)
+        weave(4, act)
+        for c in range(1, 5):
+            second_layer(c)
+        for c, copy in enumerate([act, act, dve, act, dve]):
+            store(c, copy)

@@ -54,8 +54,8 @@ def tile_picked_unet_relu_p_kernel(tc, x_words, x_scales, w1, w2, skip, offs, ce
 
         nc.sync.dma_start(xs[0:32, :].bitcast(I32), x_scales.rearrange("s q n -> (s q) n").bitcast(I32))
         nc.sync.dma_start(offs_t[:], offs)
-        nc.sync.dma_start(cell_t[:], cell)
         load_w1(0)
+        nc.sync.dma_start(cell_t[:], cell)
         load_words(0)
         load_w1(1)
         nc.vector.tensor_copy(picked_scales[:], xs[:].indirect(offs_t[:]))
@@ -182,7 +182,7 @@ def tile_picked_unet_relu_p_kernel(tc, x_words, x_scales, w1, w2, skip, offs, ce
 
         def weave(c, copy):
             grouped[c] = sb.tile([P, edges[c + 1] - edges[c], PACK], BF16, name=f"grouped{c}", align_bytes=64)
-            copy(grouped[c][:], zb[:, :, chunk_cols[c]].rearrange("p t v -> p v t"))
+            copy(grouped[c][:].rearrange("p (c i) t -> p c t i", i=4), zb[:, :, chunk_cols[c]].rearrange("p t (c i) -> p c t i", i=4))
 
         def second_layer(c):
             width = edges[c + 1] - edges[c]

@@ -52,9 +52,9 @@ def tile_picked_unet_relu_p_kernel(tc, x_words, x_scales, w1, w2, skip, offs, ce
             row = 16 * s + 4 * q
             nc.sync.dma_start(planes[s][32 * q + 4 * s : 32 * q + 4 * s + 4, :].bitcast(I32), picked_scales[row : row + 4, :].bitcast(I32))
 
-        nc.sync.dma_start(xs[0:32, :].bitcast(I32), x_scales.rearrange("s q n -> (s q) n").bitcast(I32))
-        nc.sync.dma_start(offs_t[:], offs)
         load_w1(0)
+        nc.scalar.dma_start(xs[0:32, :].bitcast(I32), x_scales.rearrange("s q n -> (s q) n").bitcast(I32))
+        nc.sync.dma_start(offs_t[:], offs)
         nc.sync.dma_start(cell_t[:], cell)
         load_words(0)
         load_w1(1)
@@ -70,7 +70,10 @@ def tile_picked_unet_relu_p_kernel(tc, x_words, x_scales, w1, w2, skip, offs, ce
         window = []
         for t in range(PACK):
             win = sb.tile([P, U], F32, name=f"window{t}", align_bytes=64)
-            nc.vector.memset(win[:], 0.0)
+            if t < 2:
+                nc.vector.memset(win[:], 0.0)
+            else:
+                nc.scalar.copy(win[:], window[0][:])
             window.append(win)
 
         act, dve = nc.scalar.copy, nc.vector.tensor_copy
@@ -133,7 +136,7 @@ def tile_picked_unet_relu_p_kernel(tc, x_words, x_scales, w1, w2, skip, offs, ce
         hs = {}
 
         def relu(t, j0, j1, on_vector=False):
-            hs[t, j0] = sb.tile([P, j1 - j0], F32, name=f"hs{t}_{j0}", align_bytes=64)
+            hs[t, j0] = sb.tile([P, j1 - j0], F32, name=f"hs{t}_{j0}", tag=f"hs{t}_{j0}", align_bytes=64)
             if on_vector:
                 nc.vector.tensor_scalar_max(hs[t, j0][:], accs[t, j0][:], 0.0)
             else:
@@ -155,12 +158,7 @@ def tile_picked_unet_relu_p_kernel(tc, x_words, x_scales, w1, w2, skip, offs, ce
         scatter_v(0, 0, P, hs[0, 0][:])
         scatter_s(1, 0, P, hs[1, 0][:])
         relu(0, P, S, True)
-        w2_b = sb.tile([P, N, PACK], BF16, name="w2b", align_bytes=64)
-        dve(w2_b[:], w2_raw[:].rearrange("p j n -> p n j"))
         scatter_v(0, P, S, hs[0, P][:])
-        w2_codes = sb.tile([P, N], U32, name="w2c", align_bytes=64)
-        w2_scales = sb.tile([P, N], U8, name="w2s", align_bytes=64)
-        nc.vector.quantize_mx(out=w2_codes[:].bitcast(FP8X4), scales=w2_scales[:], in_=w2_b[:].rearrange("p n j -> p (n j)"))
         relu(1, P, S)
         relu(2, 0, S)
         relu(3, 0, S)
@@ -172,6 +170,8 @@ def tile_picked_unet_relu_p_kernel(tc, x_words, x_scales, w1, w2, skip, offs, ce
         scatter_s(2, 0, SHARE, hs[2, 0][:, 0:SHARE])
         scatter_s(3, S_HALF, S, hs[3, 0][:, S_HALF:S])
         add_plane(2)
+        w2_b = sb.tile([P, N, PACK], BF16, name="w2b", tag="hs3_0", align_bytes=64)
+        act(w2_b[:], w2_raw[:].rearrange("p j n -> p n j"))
         edges = [0, 256, 512, 768, 896, 1024]
         chunk_cols = [slice(v0, v1) for v0, v1 in zip(edges, edges[1:])]
         grouped, accs_out = {}, {}
@@ -208,6 +208,9 @@ def tile_picked_unet_relu_p_kernel(tc, x_words, x_scales, w1, w2, skip, offs, ce
         add_last(0, 1)
         add_last(1, 2)
         add_last(2, 5)
+        w2_codes = sb.tile([P, N], U32, name="w2c", tag="w1raw1", align_bytes=64)
+        w2_scales = sb.tile([P, N], U8, name="w2s", align_bytes=64)
+        nc.vector.quantize_mx(out=w2_codes[:].bitcast(FP8X4), scales=w2_scales[:], in_=w2_b[:].rearrange("p n j -> p (n j)"))
         weave(0, act)
         weave(1, dve)
         weave(2, act)

@@ -20,7 +20,7 @@ PACK = 4
 K_PASS = P * PACK
 PASSES = K // K_PASS
 S_HALF = S // 2
-SHARE = 224
+SHARE = 192
 
 
 def tile_picked_unet_relu_p_kernel(tc, x_words, x_scales, w1, w2, skip, offs, cell, out):
@@ -52,9 +52,9 @@ def tile_picked_unet_relu_p_kernel(tc, x_words, x_scales, w1, w2, skip, offs, ce
             row = 16 * s + 4 * q
             nc.sync.dma_start(planes[s][32 * q + 4 * s : 32 * q + 4 * s + 4, :].bitcast(I32), picked_scales[row : row + 4, :].bitcast(I32))
 
-        load_w1(0)
-        nc.scalar.dma_start(xs[0:32, :].bitcast(I32), x_scales.rearrange("s q n -> (s q) n").bitcast(I32))
+        nc.sync.dma_start(xs[0:32, :].bitcast(I32), x_scales.rearrange("s q n -> (s q) n").bitcast(I32))
         nc.sync.dma_start(offs_t[:], offs)
+        load_w1(0)
         nc.sync.dma_start(cell_t[:], cell)
         load_words(0)
         load_w1(1)

@@ -27,11 +27,12 @@ def tile_picked_unet_relu_p_kernel(tc, x_words, x_scales, w1, w2, skip, offs, ce
     nc = tc.nc
     with ExitStack() as ctx:
         sb = ctx.enter_context(tc.tile_pool(name="sb", bufs=1))
+        laid = ctx.enter_context(tc.tile_pool(name="laid", bufs=1))
         ps = ctx.enter_context(tc.psum_pool(name="ps", bufs=1))
 
         offs_t = sb.tile([P, S // 16], U16, name="offs_t")
         cell_t = sb.tile([P, S // 16], U16, name="cell_t")
-        xs = sb.tile([P, T], U8, name="xs", tag="x_late", align_bytes=64)
+        xs = laid.tile([P, T], U8, name="xs", offset=4 * T - T // 2, align_bytes=64)
         w1_raw = [sb.tile([P, PACK, H], F32, name=f"w1raw{s}", tag=f"w1raw{s}", align_bytes=64) for s in range(PASSES)]
         xw = [sb.tile([P, T], I32, name="xw0", tag="xw0", align_bytes=64)]
         planes = [sb.tile([P, S], U8, name=f"plane{s}", align_bytes=64) for s in range(PASSES)]
@@ -42,8 +43,8 @@ def tile_picked_unet_relu_p_kernel(tc, x_words, x_scales, w1, w2, skip, offs, ce
         for s in range(PASSES):
             nc.gpsimd.memset(planes[s][:].bitcast(I32), 0)
 
-        def load_w1(s):
-            nc.sync.dma_start(w1_raw[s][:], w1[K_PASS * s : K_PASS * (s + 1), :].rearrange("(p j) c -> p j c", j=PACK))
+        def load_w1(s, j0=0, j1=PACK):
+            nc.sync.dma_start(w1_raw[s][:, j0:j1, :], w1[K_PASS * s : K_PASS * (s + 1), :].rearrange("(p j) c -> p j c", j=PACK)[:, j0:j1, :])
 
         def load_words(s):
             nc.sync.dma_start(xw[s][:], x_words[s].rearrange("p n t -> p (n t)").bitcast(I32))
@@ -52,19 +53,19 @@ def tile_picked_unet_relu_p_kernel(tc, x_words, x_scales, w1, w2, skip, offs, ce
             row = 16 * s + 4 * q
             nc.sync.dma_start(planes[s][32 * q + 4 * s : 32 * q + 4 * s + 4, :].bitcast(I32), picked_scales[row : row + 4, :].bitcast(I32))
 
+        load_w1(0, 0, 2)
         nc.sync.dma_start(xs[0:32, :].bitcast(I32), x_scales.rearrange("s q n -> (s q) n").bitcast(I32))
         nc.sync.dma_start(offs_t[:], offs)
-        load_w1(0)
+        load_w1(0, 2, PACK)
         nc.sync.dma_start(cell_t[:], cell)
         load_words(0)
         load_w1(1)
         nc.vector.tensor_copy(picked_scales[:], xs[:].indirect(offs_t[:]))
         for q in range(4):
             place_scales(0, q)
-        place_scales(1, 0)
-        xw.append(sb.tile([P, T], I32, name="xw1", tag="x_late", align_bytes=64))
+        xw.append(laid.tile([P, T], I32, name="xw1", offset=0, align_bytes=64))
         load_words(1)
-        for q in range(1, 4):
+        for q in range(4):
             place_scales(1, q)
 
         window = []
@@ -83,7 +84,10 @@ def tile_picked_unet_relu_p_kernel(tc, x_words, x_scales, w1, w2, skip, offs, ce
         def quantise_w1(s):
             src = w1_raw[s][:].rearrange("p j (b a e r) -> p a e b r j", a=2, e=2, r=8)
             for a, cast in enumerate([dve, act]):
-                wb = sb.tile([P, 2, P, PACK], BF16, name=f"w1b{s}_{a}", tag=f"w1b{s}_{a}", align_bytes=64)
+                if (s, a) == (0, 0):
+                    wb = laid.tile([P, 2, P, PACK], BF16, name="w1b0_0", offset=4 * T, align_bytes=64)
+                else:
+                    wb = sb.tile([P, 2, P, PACK], BF16, name=f"w1b{s}_{a}", align_bytes=64)
                 cast(wb[:].rearrange("p e (b r) j -> p e b r j", r=8), src[:, a])
                 codes = sb.tile([P, 2 * P], U32, name=f"w1c{s}_{a}", align_bytes=64)
                 scales = sb.tile([P, 2 * P], U8, name=f"w1s{s}_{a}", align_bytes=64)
@@ -125,12 +129,15 @@ def tile_picked_unet_relu_p_kernel(tc, x_words, x_scales, w1, w2, skip, offs, ce
 
         skip_planes = skip.rearrange("(b t r) v -> t b r v", t=PACK, r=8)
         w2_planes = w2.rearrange("(b t r) n -> t b r n", t=PACK, r=8)
-        w2_raw = sb.tile([P, PACK, N], F32, name="w2raw", tag="w1b0_0", align_bytes=64)
+        w2_raw = laid.tile([P, PACK, N], F32, name="w2raw", offset=4 * T, align_bytes=64)
         for t in range(PACK):
             nc.sync.dma_start(w2_raw[:, t, :], w2_planes[t])
         skip_t = []
         for t, slot in enumerate(["w1raw0", "xw0", "w1raw1", "x_late"]):
-            skip_t.append(sb.tile([P, U], F32, name=f"skip{t}", tag=slot, align_bytes=64))
+            if slot == "x_late":
+                skip_t.append(laid.tile([P, U], F32, name=f"skip{t}", offset=0, align_bytes=64))
+            else:
+                skip_t.append(sb.tile([P, U], F32, name=f"skip{t}", tag=slot, align_bytes=64))
             nc.sync.dma_start(skip_t[t][:], skip_planes[t])
 
         hs = {}

@@ -63,9 +63,11 @@ def tile_picked_unet_relu_p_kernel(tc, x_words, x_scales, w1, w2, skip, offs, ce
         nc.vector.tensor_copy(picked_scales[:], xs[:].indirect(offs_t[:]))
         for q in range(4):
             place_scales(0, q)
+        for q in range(2):
+            place_scales(1, q)
         xw.append(laid.tile([P, T], I32, name="xw1", offset=0, align_bytes=64))
         load_words(1)
-        for q in range(4):
+        for q in range(2, 4):
             place_scales(1, q)
 
         window = []

@@ -1,6 +1,7 @@
 from contextlib import ExitStack
 
 import concourse.mybir as mybir
+from concourse.masks import make_identity
 
 K, T, S, H, N, U = 1024, 2048, 512, 512, 128, 1024
 FLOPS = 2 * K * H * S + 2 * H * N * U
@@ -19,8 +20,9 @@ P = 128
 PACK = 4
 K_PASS = P * PACK
 PASSES = K // K_PASS
-S_HALF = S // 2
-SHARE = 192
+S_HALF = 320
+SHARE = 160
+TURNED = 512
 
 
 def tile_picked_unet_relu_p_kernel(tc, x_words, x_scales, w1, w2, skip, offs, cell, out):
@@ -42,6 +44,9 @@ def tile_picked_unet_relu_p_kernel(tc, x_words, x_scales, w1, w2, skip, offs, ce
         nc.gpsimd.memset(xs[64:128, :].bitcast(I32), 0)
         for s in range(PASSES):
             nc.gpsimd.memset(planes[s][:].bitcast(I32), 0)
+
+        ident = sb.tile([P, P], F32, name="ident", align_bytes=64)
+        make_identity(nc, ident[:])
 
         def load_w1(s, j0=0, j1=PACK):
             nc.sync.dma_start(w1_raw[s][:, j0:j1, :], w1[K_PASS * s : K_PASS * (s + 1), :].rearrange("(p j) c -> p j c", j=PACK)[:, j0:j1, :])
@@ -157,10 +162,41 @@ def tile_picked_unet_relu_p_kernel(tc, x_words, x_scales, w1, w2, skip, offs, ce
         def scatter_s(t, j0, j1, src):
             nc.scalar.activation(out=window[t][:].indirect(cell_t[:, j0 // 16 : j1 // 16]), in_=src, func=ACT.Copy)
 
-        zb = sb.tile([P, PACK, U], BF16, name="zb", align_bytes=64)
+        def add_plane(t, v0=TURNED, v1=U):
+            nc.vector.tensor_tensor(zb[:, t, v0 - TURNED : v1 - TURNED], window[t][:, v0:v1], skip_t[t][:, v0:v1], ALU.add)
 
-        def add_plane(t):
-            nc.vector.tensor_tensor(zb[:, t, :], window[t][:], skip_t[t][:], ALU.add)
+        sums, back, grouped = {}, {}, {}
+
+        def turn(u, source, e):
+            for c in range(2):
+                if (u, c) not in sums:
+                    sums[u, c] = ps.tile([P, 2, 2, P], F32, name=f"sum{u}{c}", tag=f"bank{[5, 4, 0, 1][2 * u + c]}")
+                for blk in range(2):
+                    v0 = 2 * P * c + P * blk
+                    nc.tensor.matmul(
+                        sums[u, c][:, blk, e, :],
+                        lhsT=source[2 * u + e][:, v0 : v0 + P],
+                        rhs=ident[:],
+                        is_transpose=True,
+                        start=(source is skip_t and e == 0 and blk == 0),
+                        stop=(source is window and e == 1 and blk == 1),
+                    )
+
+        def turn_back(u, c, copy):
+            pairs = sb.tile([P, 2, P, 2], BF16, name=f"pairs{u}{c}", tag=f"pairs{u}{c}", align_bytes=64)
+            copy(pairs[:], sums[u, c][:].rearrange("v b e p -> v b p e"))
+            if u == 0:
+                back[c] = ps.tile([P, 2, 2 * P], F32, name=f"back{c}", tag=f"bank{2 + c}")
+            words = pairs[:].rearrange("v b p e -> v b (p e)").bitcast(F32)
+            for blk in range(2):
+                nc.tensor.transpose(back[c][:, u, P * blk : P * (blk + 1)], words[:, blk, :], ident[:])
+
+        def join(c, copy):
+            half, v0 = divmod(edges[c], 2 * P)
+            width = edges[c + 1] - edges[c]
+            grouped[c] = sb.tile([P, width, PACK], BF16, name=f"grouped{c}", align_bytes=64)
+            words = grouped[c][:].rearrange("p v t -> p (v t)").bitcast(F32).rearrange("p (v u) -> p v u", u=2)
+            copy(words, back[half][:, :, v0 : v0 + width].rearrange("p u v -> p v u"))
 
         relu(1, 0, P)
         relu(0, 0, P)
@@ -173,32 +209,39 @@ def tile_picked_unet_relu_p_kernel(tc, x_words, x_scales, w1, w2, skip, offs, ce
         relu(3, 0, S)
         scatter_s(1, P, S, hs[1, P][:])
         scatter_v(2, SHARE, S, hs[2, 0][:, SHARE:S])
+        turn(0, skip_t, 0)
+        turn(0, skip_t, 1)
+        turn(0, window, 0)
+        turn(0, window, 1)
+        turn(1, skip_t, 0)
+        turn(1, skip_t, 1)
+        turn_back(0, 0, dve)
+        turn_back(0, 1, dve)
+        zb = sb.tile([P, PACK, U - TURNED], BF16, name="zb", tag="pairs00", align_bytes=64)
         add_plane(0)
         add_plane(1)
         scatter_s(3, 0, S_HALF, hs[3, 0][:, 0:S_HALF])
         scatter_s(2, 0, SHARE, hs[2, 0][:, 0:SHARE])
         scatter_s(3, S_HALF, S, hs[3, 0][:, S_HALF:S])
         add_plane(2)
+        turn(1, window, 0)
+        turn(1, window, 1)
         w2_b = sb.tile([P, N, PACK], BF16, name="w2b", tag="hs3_0", align_bytes=64)
         act(w2_b[:], w2_raw[:].rearrange("p j n -> p n j"))
-        edges = [0, 256, 512, 768, 896, 1024]
+        edges = [0, 256, 384, 512, 768, 1024]
         chunk_cols = [slice(v0, v1) for v0, v1 in zip(edges, edges[1:])]
-        grouped, accs_out = {}, {}
-
-        def add_last(c0, c1):
-            cols = slice(edges[c0], edges[c1])
-            nc.vector.tensor_tensor(zb[:, 3, cols], window[3][:, cols], skip_t[3][:, cols], ALU.add)
+        accs_out = {}
 
         def weave(c, copy):
             grouped[c] = sb.tile([P, edges[c + 1] - edges[c], PACK], BF16, name=f"grouped{c}", align_bytes=64)
-            copy(grouped[c][:].rearrange("p (c i) t -> p c t i", i=4), zb[:, :, chunk_cols[c]].rearrange("p t (c i) -> p c t i", i=4))
+            copy(grouped[c][:].rearrange("p (c i) t -> p c t i", i=4), zb[:, :, edges[c] - TURNED : edges[c + 1] - TURNED].rearrange("p t (c i) -> p c t i", i=4))
 
         def second_layer(c):
             width = edges[c + 1] - edges[c]
             codes = sb.tile([P, width], U32, name=f"zc{c}", align_bytes=64)
             scales = sb.tile([P, width], U8, name=f"zs{c}", align_bytes=64)
             nc.vector.quantize_mx(out=codes[:].bitcast(FP8X4), scales=scales[:], in_=grouped[c][:].rearrange("p v t -> p (v t)"))
-            accs_out[c] = ps.tile([P, width], F32, name=f"o{c}", tag=f"bank{c}")
+            accs_out[c] = ps.tile([P, width], F32, name=f"o{c}", tag=f"bank{[6, 7, 4, 1, 0][c]}")
             nc.tensor.matmul_mx(
                 out=accs_out[c][:],
                 lhsT=w2_codes[:].bitcast(FP8X4),
@@ -214,19 +257,18 @@ def tile_picked_unet_relu_p_kernel(tc, x_words, x_scales, w1, w2, skip, offs, ce
             copy(res[:], accs_out[c][:])
             nc.sync.dma_start(out[:, chunk_cols[c]], res[:])
 
-        add_last(0, 1)
-        add_last(1, 2)
-        add_last(2, 5)
+        add_plane(3, 512, 768)
+        add_plane(3, 768, U)
+        turn_back(1, 0, act)
+        turn_back(1, 1, act)
         w2_codes = sb.tile([P, N], U32, name="w2c", tag="w1raw1", align_bytes=64)
         w2_scales = sb.tile([P, N], U8, name="w2s", align_bytes=64)
         nc.vector.quantize_mx(out=w2_codes[:].bitcast(FP8X4), scales=w2_scales[:], in_=w2_b[:].rearrange("p n j -> p (n j)"))
-        weave(0, act)
-        weave(1, dve)
-        weave(2, act)
-        second_layer(0)
         weave(3, dve)
-        weave(4, act)
-        for c in range(1, 5):
+        weave(4, dve)
+        for c in range(3):
+            join(c, act)
+        for c in (3, 4, 0, 1, 2):
             second_layer(c)
-        for c, copy in enumerate([act, act, dve, act, dve]):
+        for c, copy in ((3, act), (4, act), (0, act), (1, act), (2, dve)):
             store(c, copy)

@@ -35,8 +35,8 @@ def tile_picked_unet_relu_p_kernel(tc, x_words, x_scales, w1, w2, skip, offs, ce
         offs_t = sb.tile([P, S // 16], U16, name="offs_t")
         cell_t = sb.tile([P, S // 16], U16, name="cell_t")
         xs = laid.tile([P, T], U8, name="xs", offset=4 * T - T // 2, align_bytes=64)
-        w1_raw = [sb.tile([P, PACK, H], F32, name=f"w1raw{s}", tag=f"w1raw{s}", align_bytes=64) for s in range(PASSES)]
-        xw = [sb.tile([P, T], I32, name="xw0", tag="xw0", align_bytes=64)]
+        w1_raw = [sb.tile([P, PACK, H], F32, name=f"w1raw{s}", tag=f"w1raw{s}", align_bytes=256) for s in range(PASSES)]
+        xw = [sb.tile([P, T], I32, name="xw0", tag="xw0", align_bytes=256)]
         planes = [sb.tile([P, S], U8, name=f"plane{s}", align_bytes=64) for s in range(PASSES)]
         picked_scales = sb.tile([P, S], U8, name="picked_scales", align_bytes=64)
 
@@ -70,7 +70,7 @@ def tile_picked_unet_relu_p_kernel(tc, x_words, x_scales, w1, w2, skip, offs, ce
             place_scales(0, q)
         for q in range(2):
             place_scales(1, q)
-        xw.append(laid.tile([P, T], I32, name="xw1", offset=0, align_bytes=64))
+        xw.append(laid.tile([P, T], I32, name="xw1", offset=0, align_bytes=256))
         load_words(1)
         for q in range(2, 4):
             place_scales(1, q)
@@ -136,15 +136,15 @@ def tile_picked_unet_relu_p_kernel(tc, x_words, x_scales, w1, w2, skip, offs, ce
 
         skip_planes = skip.rearrange("(b t r) v -> t b r v", t=PACK, r=8)
         w2_planes = w2.rearrange("(b t r) n -> t b r n", t=PACK, r=8)
-        w2_raw = laid.tile([P, PACK, N], F32, name="w2raw", offset=4 * T, align_bytes=64)
+        w2_raw = laid.tile([P, PACK, N], F32, name="w2raw", offset=4 * T, align_bytes=256)
         for t in range(PACK):
             nc.sync.dma_start(w2_raw[:, t, :], w2_planes[t])
         skip_t = []
         for t, slot in enumerate(["w1raw0", "xw0", "w1raw1", "x_late"]):
             if slot == "x_late":
-                skip_t.append(laid.tile([P, U], F32, name=f"skip{t}", offset=0, align_bytes=64))
+                skip_t.append(laid.tile([P, U], F32, name=f"skip{t}", offset=0, align_bytes=256))
             else:
-                skip_t.append(sb.tile([P, U], F32, name=f"skip{t}", tag=slot, align_bytes=64))
+                skip_t.append(sb.tile([P, U], F32, name=f"skip{t}", tag=slot, align_bytes=256))
             nc.sync.dma_start(skip_t[t][:], skip_planes[t])
 
         hs = {}
@@ -253,7 +253,7 @@ def tile_picked_unet_relu_p_kernel(tc, x_words, x_scales, w1, w2, skip, offs, ce
             )
 
         def store(c, copy):
-            res = sb.tile([P, edges[c + 1] - edges[c]], F32, name=f"res{c}", align_bytes=64)
+            res = sb.tile([P, edges[c + 1] - edges[c]], F32, name=f"res{c}", align_bytes=256)
             copy(res[:], accs_out[c][:])
             nc.sync.dma_start(out[:, chunk_cols[c]], res[:])
 
@@ -261,7 +261,7 @@ def tile_picked_unet_relu_p_kernel(tc, x_words, x_scales, w1, w2, skip, offs, ce
         add_plane(3, 768, U)
         turn_back(1, 0, act)
         turn_back(1, 1, act)
-        w2_codes = sb.tile([P, N], U32, name="w2c", tag="w1raw1", align_bytes=64)
+        w2_codes = sb.tile([P, N], U32, name="w2c", tag="w1raw1", align_bytes=256)
         w2_scales = sb.tile([P, N], U8, name="w2s", align_bytes=64)
         nc.vector.quantize_mx(out=w2_codes[:].bitcast(FP8X4), scales=w2_scales[:], in_=w2_b[:].rearrange("p n j -> p (n j)"))
         weave(3, dve)

@@ -40,8 +40,7 @@ def tile_picked_unet_relu_p_kernel(tc, x_words, x_scales, w1, w2, skip, offs, ce
         planes = [sb.tile([P, S], U8, name=f"plane{s}", align_bytes=64) for s in range(PASSES)]
         picked_scales = sb.tile([P, S], U8, name="picked_scales", align_bytes=64)
 
-        nc.gpsimd.memset(xs[32:64, :].bitcast(I32), 0)
-        nc.gpsimd.memset(xs[64:128, :].bitcast(I32), 0)
+        nc.gpsimd.memset(xs[:].bitcast(I32), 0)
         for s in range(PASSES):
             nc.gpsimd.memset(planes[s][:].bitcast(I32), 0)
 
@@ -55,11 +54,11 @@ def tile_picked_unet_relu_p_kernel(tc, x_words, x_scales, w1, w2, skip, offs, ce
             nc.sync.dma_start(xw[s][:], x_words[s].rearrange("p n t -> p (n t)").bitcast(I32))
 
         def place_scales(s, q):
-            row = 16 * s + 4 * q
-            nc.sync.dma_start(planes[s][32 * q + 4 * s : 32 * q + 4 * s + 4, :].bitcast(I32), picked_scales[row : row + 4, :].bitcast(I32))
+            row = 4 * (16 * s + 4 * q)
+            nc.sync.dma_start(planes[s][32 * q + 4 * s : 32 * q + 4 * s + 4, :].bitcast(I32), picked_scales[row : row + 16 : 4, :].bitcast(I32))
 
         load_w1(0, 0, 2)
-        nc.sync.dma_start(xs[0:32, :].bitcast(I32), x_scales.rearrange("s q n -> (s q) n").bitcast(I32))
+        nc.sync.dma_start(xs[0:P:4, :].bitcast(I32), x_scales.rearrange("s q n -> (s q) n").bitcast(I32))
         nc.sync.dma_start(offs_t[:], offs)
         load_w1(0, 2, PACK)
         nc.sync.dma_start(cell_t[:], cell)

@@ -88,13 +88,13 @@ def tile_picked_unet_relu_p_kernel(tc, x_words, x_scales, w1, w2, skip, offs, ce
         w1_codes, w1_scales = {}, {}
 
         def quantise_w1(s):
-            src = w1_raw[s][:].rearrange("p j (b a e r) -> p a e b r j", a=2, e=2, r=8)
+            src = w1_raw[s][:].rearrange("p j (m a e) -> p a m e j", a=2, e=2)
             for a, cast in enumerate([dve, act]):
                 if (s, a) == (0, 0):
                     wb = laid.tile([P, 2, P, PACK], BF16, name="w1b0_0", offset=4 * T, align_bytes=64)
                 else:
                     wb = sb.tile([P, 2, P, PACK], BF16, name=f"w1b{s}_{a}", align_bytes=64)
-                cast(wb[:].rearrange("p e (b r) j -> p e b r j", r=8), src[:, a])
+                cast(wb[:].rearrange("p e m j -> p m e j"), src[:, a])
                 codes = sb.tile([P, 2 * P], U32, name=f"w1c{s}_{a}", align_bytes=64)
                 scales = sb.tile([P, 2 * P], U8, name=f"w1s{s}_{a}", align_bytes=64)
                 nc.vector.quantize_mx(out=codes[:].bitcast(FP8X4), scales=scales[:], in_=wb[:].rearrange("p e m j -> p (e m j)"))
@@ -133,11 +133,9 @@ def tile_picked_unet_relu_p_kernel(tc, x_words, x_scales, w1, w2, skip, offs, ce
         for t, j0, j1 in pieces:
             first_pass(accs[t, j0], t, 1, j0, j1)
 
-        skip_planes = skip.rearrange("(b t r) v -> t b r v", t=PACK, r=8)
-        w2_planes = w2.rearrange("(b t r) n -> t b r n", t=PACK, r=8)
+        skip_planes = skip.rearrange("(p t) v -> t p v", t=PACK)
         w2_raw = laid.tile([P, PACK, N], F32, name="w2raw", offset=4 * T, align_bytes=256)
-        for t in range(PACK):
-            nc.sync.dma_start(w2_raw[:, t, :], w2_planes[t])
+        nc.sync.dma_start(w2_raw[:], w2.rearrange("(p t) n -> p t n", t=PACK))
         skip_t = []
         for t, slot in enumerate(["w1raw0", "xw0", "w1raw1", "x_late"]):
             if slot == "x_late":

@@ -34,17 +34,17 @@ def tile_picked_unet_relu_p_kernel(tc, x_words, x_scales, w1, w2, skip, offs, ce
 
         offs_t = sb.tile([P, S // 16], U16, name="offs_t")
         cell_t = sb.tile([P, S // 16], U16, name="cell_t")
-        xs = laid.tile([P, T], U8, name="xs", offset=4 * T - T // 2, align_bytes=64)
+        xs = laid.tile([P, T], U8, name="xs", offset=4 * T - T // 2, align_bytes=256)
         w1_raw = [sb.tile([P, PACK, H], F32, name=f"w1raw{s}", tag=f"w1raw{s}", align_bytes=256) for s in range(PASSES)]
         xw = [sb.tile([P, T], I32, name="xw0", tag="xw0", align_bytes=256)]
-        planes = [sb.tile([P, S], U8, name=f"plane{s}", align_bytes=64) for s in range(PASSES)]
-        picked_scales = sb.tile([P, S], U8, name="picked_scales", align_bytes=64)
+        planes = [sb.tile([P, S], U8, name=f"plane{s}", align_bytes=256) for s in range(PASSES)]
+        picked_scales = sb.tile([P, S], U8, name="picked_scales", align_bytes=256)
 
         nc.gpsimd.memset(xs[:].bitcast(I32), 0)
         for s in range(PASSES):
             nc.gpsimd.memset(planes[s][:].bitcast(I32), 0)
 
-        ident = sb.tile([P, P], F32, name="ident", align_bytes=64)
+        ident = sb.tile([P, P], F32, name="ident", align_bytes=256)
         make_identity(nc, ident[:])
 
         def load_w1(s, j0=0, j1=PACK):
@@ -76,7 +76,7 @@ def tile_picked_unet_relu_p_kernel(tc, x_words, x_scales, w1, w2, skip, offs, ce
 
         window = []
         for t in range(PACK):
-            win = sb.tile([P, U], F32, name=f"window{t}", align_bytes=64)
+            win = sb.tile([P, U], F32, name=f"window{t}", align_bytes=256)
             if t < 2:
                 nc.vector.memset(win[:], 0.0)
             else:
@@ -91,18 +91,18 @@ def tile_picked_unet_relu_p_kernel(tc, x_words, x_scales, w1, w2, skip, offs, ce
             src = w1_raw[s][:].rearrange("p j (m a e) -> p a m e j", a=2, e=2)
             for a, cast in enumerate([dve, act]):
                 if (s, a) == (0, 0):
-                    wb = laid.tile([P, 2, P, PACK], BF16, name="w1b0_0", offset=4 * T, align_bytes=64)
+                    wb = laid.tile([P, 2, P, PACK], BF16, name="w1b0_0", offset=4 * T, align_bytes=256)
                 else:
-                    wb = sb.tile([P, 2, P, PACK], BF16, name=f"w1b{s}_{a}", align_bytes=64)
+                    wb = sb.tile([P, 2, P, PACK], BF16, name=f"w1b{s}_{a}", align_bytes=256)
                 cast(wb[:].rearrange("p e m j -> p m e j"), src[:, a])
-                codes = sb.tile([P, 2 * P], U32, name=f"w1c{s}_{a}", align_bytes=64)
-                scales = sb.tile([P, 2 * P], U8, name=f"w1s{s}_{a}", align_bytes=64)
+                codes = sb.tile([P, 2 * P], U32, name=f"w1c{s}_{a}", align_bytes=256)
+                scales = sb.tile([P, 2 * P], U8, name=f"w1s{s}_{a}", align_bytes=256)
                 nc.vector.quantize_mx(out=codes[:].bitcast(FP8X4), scales=scales[:], in_=wb[:].rearrange("p e m j -> p (e m j)"))
                 for e in range(2):
                     w1_codes[s, 2 * a + e] = codes[:, P * e : P * (e + 1)]
                     w1_scales[s, 2 * a + e] = scales[:, P * e : P * (e + 1)]
 
-        picked_words = [sb.tile([P, S], U32, name=f"picked_words{s}", align_bytes=64) for s in range(PASSES)]
+        picked_words = [sb.tile([P, S], U32, name=f"picked_words{s}", align_bytes=256) for s in range(PASSES)]
 
         def gather_words(s, j0, j1):
             nc.vector.tensor_copy(picked_words[s][:, j0:j1], xw[s][:].bitcast(U32).indirect(offs_t[:, j0 // 16 : j1 // 16]))
@@ -147,7 +147,7 @@ def tile_picked_unet_relu_p_kernel(tc, x_words, x_scales, w1, w2, skip, offs, ce
         hs = {}
 
         def relu(t, j0, j1, on_vector=False):
-            hs[t, j0] = sb.tile([P, j1 - j0], F32, name=f"hs{t}_{j0}", tag=f"hs{t}_{j0}", align_bytes=64)
+            hs[t, j0] = sb.tile([P, j1 - j0], F32, name=f"hs{t}_{j0}", tag=f"hs{t}_{j0}", align_bytes=256)
             if on_vector:
                 nc.vector.tensor_scalar_max(hs[t, j0][:], accs[t, j0][:], 0.0)
             else:
@@ -180,7 +180,7 @@ def tile_picked_unet_relu_p_kernel(tc, x_words, x_scales, w1, w2, skip, offs, ce
                     )
 
         def turn_back(u, c, copy):
-            pairs = sb.tile([P, 2, P, 2], BF16, name=f"pairs{u}{c}", tag=f"pairs{u}{c}", align_bytes=64)
+            pairs = sb.tile([P, 2, P, 2], BF16, name=f"pairs{u}{c}", tag=f"pairs{u}{c}", align_bytes=256)
             copy(pairs[:], sums[u, c][:].rearrange("v b e p -> v b p e"))
             if u == 0:
                 back[c] = ps.tile([P, 2, 2 * P], F32, name=f"back{c}", tag=f"bank{2 + c}")
@@ -191,7 +191,7 @@ def tile_picked_unet_relu_p_kernel(tc, x_words, x_scales, w1, w2, skip, offs, ce
         def join(c, copy):
             half, v0 = divmod(edges[c], 2 * P)
             width = edges[c + 1] - edges[c]
-            grouped[c] = sb.tile([P, width, PACK], BF16, name=f"grouped{c}", align_bytes=64)
+            grouped[c] = sb.tile([P, width, PACK], BF16, name=f"grouped{c}", align_bytes=256)
             words = grouped[c][:].rearrange("p v t -> p (v t)").bitcast(F32).rearrange("p (v u) -> p v u", u=2)
             copy(words, back[half][:, :, v0 : v0 + width].rearrange("p u v -> p v u"))
 
@@ -214,7 +214,7 @@ def tile_picked_unet_relu_p_kernel(tc, x_words, x_scales, w1, w2, skip, offs, ce
         turn(1, skip_t, 1)
         turn_back(0, 0, dve)
         turn_back(0, 1, dve)
-        zb = sb.tile([P, PACK, U - TURNED], BF16, name="zb", tag="pairs00", align_bytes=64)
+        zb = sb.tile([P, PACK, U - TURNED], BF16, name="zb", tag="pairs00", align_bytes=256)
         add_plane(0)
         add_plane(1)
         scatter_s(3, 0, S_HALF, hs[3, 0][:, 0:S_HALF])
@@ -223,20 +223,20 @@ def tile_picked_unet_relu_p_kernel(tc, x_words, x_scales, w1, w2, skip, offs, ce
         add_plane(2)
         turn(1, window, 0)
         turn(1, window, 1)
-        w2_b = sb.tile([P, N, PACK], BF16, name="w2b", tag="hs3_0", align_bytes=64)
+        w2_b = sb.tile([P, N, PACK], BF16, name="w2b", tag="hs3_0", align_bytes=256)
         act(w2_b[:], w2_raw[:].rearrange("p j n -> p n j"))
         edges = [0, 256, 384, 512, 768, 1024]
         chunk_cols = [slice(v0, v1) for v0, v1 in zip(edges, edges[1:])]
         accs_out = {}
 
         def weave(c, copy):
-            grouped[c] = sb.tile([P, edges[c + 1] - edges[c], PACK], BF16, name=f"grouped{c}", align_bytes=64)
+            grouped[c] = sb.tile([P, edges[c + 1] - edges[c], PACK], BF16, name=f"grouped{c}", align_bytes=256)
             copy(grouped[c][:].rearrange("p (c i) t -> p c t i", i=4), zb[:, :, edges[c] - TURNED : edges[c + 1] - TURNED].rearrange("p t (c i) -> p c t i", i=4))
 
         def second_layer(c):
             width = edges[c + 1] - edges[c]
-            codes = sb.tile([P, width], U32, name=f"zc{c}", align_bytes=64)
-            scales = sb.tile([P, width], U8, name=f"zs{c}", align_bytes=64)
+            codes = sb.tile([P, width], U32, name=f"zc{c}", align_bytes=256)
+            scales = sb.tile([P, width], U8, name=f"zs{c}", align_bytes=256)
             nc.vector.quantize_mx(out=codes[:].bitcast(FP8X4), scales=scales[:], in_=grouped[c][:].rearrange("p v t -> p (v t)"))
             accs_out[c] = ps.tile([P, width], F32, name=f"o{c}", tag=f"bank{[6, 7, 4, 1, 0][c]}")
             nc.tensor.matmul_mx(
@@ -259,7 +259,7 @@ def tile_picked_unet_relu_p_kernel(tc, x_words, x_scales, w1, w2, skip, offs, ce
         turn_back(1, 0, act)
         turn_back(1, 1, act)
         w2_codes = sb.tile([P, N], U32, name="w2c", tag="w1raw1", align_bytes=256)
-        w2_scales = sb.tile([P, N], U8, name="w2s", align_bytes=64)
+        w2_scales = sb.tile([P, N], U8, name="w2s", align_bytes=256)
         nc.vector.quantize_mx(out=w2_codes[:].bitcast(FP8X4), scales=w2_scales[:], in_=w2_b[:].rearrange("p n j -> p (n j)"))
         weave(3, dve)
         weave(4, dve)

@@ -224,7 +224,7 @@ def tile_picked_unet_relu_p_kernel(tc, x_words, x_scales, w1, w2, skip, offs, ce
         turn(1, window, 0)
         turn(1, window, 1)
         w2_b = sb.tile([P, N, PACK], BF16, name="w2b", tag="hs3_0", align_bytes=256)
-        act(w2_b[:], w2_raw[:].rearrange("p j n -> p n j"))
+        act(w2_b[:].rearrange("p (c i) j -> p c j i", i=4), w2_raw[:].rearrange("p j (c i) -> p c j i", i=4))
         edges = [0, 256, 384, 512, 768, 1024]
         chunk_cols = [slice(v0, v1) for v0, v1 in zip(edges, edges[1:])]
         accs_out = {}

@@ -206,6 +206,8 @@ def tile_picked_unet_relu_p_kernel(tc, x_words, x_scales, w1, w2, skip, offs, ce
         relu(3, 0, S)
         scatter_s(1, P, S, hs[1, P][:])
         scatter_v(2, SHARE, S, hs[2, 0][:, SHARE:S])
+        w2_b = sb.tile([P, N, PACK], BF16, name="w2b", tag="hs0_128", align_bytes=256)
+        nc.gpsimd.tensor_copy(w2_b[:], w2_raw[:].rearrange("p j n -> p n j"))
         turn(0, skip_t, 0)
         turn(0, skip_t, 1)
         turn(0, window, 0)
@@ -223,8 +225,6 @@ def tile_picked_unet_relu_p_kernel(tc, x_words, x_scales, w1, w2, skip, offs, ce
         add_plane(2)
         turn(1, window, 0)
         turn(1, window, 1)
-        w2_b = sb.tile([P, N, PACK], BF16, name="w2b", tag="hs3_0", align_bytes=256)
-        act(w2_b[:].rearrange("p (c i) j -> p c j i", i=4), w2_raw[:].rearrange("p j (c i) -> p c j i", i=4))
         edges = [0, 256, 384, 512, 768, 1024]
         chunk_cols = [slice(v0, v1) for v0, v1 in zip(edges, edges[1:])]
         accs_out = {}

from contextlib import ExitStack

import concourse.mybir as mybir
from concourse.masks import make_identity

K, T, S, H, N, U = 1024, 2048, 512, 512, 128, 1024
FLOPS = 2 * K * H * S + 2 * H * N * U

F32 = mybir.dt.float32
BF16 = mybir.dt.bfloat16
I32 = mybir.dt.int32
U32 = mybir.dt.uint32
U16 = mybir.dt.uint16
U8 = mybir.dt.uint8
FP8X4 = mybir.dt.float8_e4m3fn_x4
ACT = mybir.ActivationFunctionType
ALU = mybir.AluOpType

P = 128
PACK = 4
K_PASS = P * PACK
PASSES = K // K_PASS
S_HALF = 320
SHARE = 160
TURNED = 512


def tile_picked_unet_relu_p_kernel(tc, x_words, x_scales, w1, w2, skip, offs, cell, out):
    nc = tc.nc
    with ExitStack() as ctx:
        sb = ctx.enter_context(tc.tile_pool(name="sb", bufs=1))
        laid = ctx.enter_context(tc.tile_pool(name="laid", bufs=1))
        ps = ctx.enter_context(tc.psum_pool(name="ps", bufs=1))

        offs_t = sb.tile([P, S // 16], U16, name="offs_t")
        cell_t = sb.tile([P, S // 16], U16, name="cell_t")
        xs = laid.tile([P, T], U8, name="xs", offset=4 * T - T // 2, align_bytes=256)
        w1_raw = [sb.tile([P, PACK, H], F32, name=f"w1raw{s}", tag=f"w1raw{s}", align_bytes=256) for s in range(PASSES)]
        xw = [sb.tile([P, T], I32, name="xw0", tag="xw0", align_bytes=256)]
        planes = [sb.tile([P, S], U8, name=f"plane{s}", align_bytes=256) for s in range(PASSES)]
        picked_scales = sb.tile([P, S], U8, name="picked_scales", align_bytes=256)

        nc.gpsimd.memset(xs[:].bitcast(I32), 0)
        for s in range(PASSES):
            nc.gpsimd.memset(planes[s][:].bitcast(I32), 0)

        ident = sb.tile([P, P], F32, name="ident", align_bytes=256)
        make_identity(nc, ident[:])

        def load_w1(s, j0=0, j1=PACK):
            nc.sync.dma_start(w1_raw[s][:, j0:j1, :], w1[K_PASS * s : K_PASS * (s + 1), :].rearrange("(p j) c -> p j c", j=PACK)[:, j0:j1, :])

        def load_words(s):
            nc.sync.dma_start(xw[s][:], x_words[s].rearrange("p n t -> p (n t)").bitcast(I32))

        def place_scales(s, q):
            row = 4 * (16 * s + 4 * q)
            nc.sync.dma_start(planes[s][32 * q + 4 * s : 32 * q + 4 * s + 4, :].bitcast(I32), picked_scales[row : row + 16 : 4, :].bitcast(I32))

        load_w1(0, 0, 2)
        nc.sync.dma_start(xs[0:P:4, :].bitcast(I32), x_scales.rearrange("s q n -> (s q) n").bitcast(I32))
        nc.sync.dma_start(offs_t[:], offs)
        load_w1(0, 2, PACK)
        nc.sync.dma_start(cell_t[:], cell)
        load_words(0)
        load_w1(1)
        nc.vector.tensor_copy(picked_scales[:], xs[:].indirect(offs_t[:]))
        for q in range(4):
            place_scales(0, q)
        for q in range(2):
            place_scales(1, q)
        xw.append(laid.tile([P, T], I32, name="xw1", offset=0, align_bytes=256))
        load_words(1)
        for q in range(2, 4):
            place_scales(1, q)

        window = []
        for t in range(PACK):
            win = sb.tile([P, U], F32, name=f"window{t}", align_bytes=256)
            if t < 2:
                nc.vector.memset(win[:], 0.0)
            else:
                nc.scalar.copy(win[:], window[0][:])
            window.append(win)

        act, dve = nc.scalar.copy, nc.vector.tensor_copy

        w1_codes, w1_scales = {}, {}

        def quantise_w1(s):
            src = w1_raw[s][:].rearrange("p j (m a e) -> p a m e j", a=2, e=2)
            for a, cast in enumerate([dve, act]):
                if (s, a) == (0, 0):
                    wb = laid.tile([P, 2, P, PACK], BF16, name="w1b0_0", offset=4 * T, align_bytes=256)
                else:
                    wb = sb.tile([P, 2, P, PACK], BF16, name=f"w1b{s}_{a}", align_bytes=256)
                cast(wb[:].rearrange("p e m j -> p m e j"), src[:, a])
                codes = sb.tile([P, 2 * P], U32, name=f"w1c{s}_{a}", align_bytes=256)
                scales = sb.tile([P, 2 * P], U8, name=f"w1s{s}_{a}", align_bytes=256)
                nc.vector.quantize_mx(out=codes[:].bitcast(FP8X4), scales=scales[:], in_=wb[:].rearrange("p e m j -> p (e m j)"))
                for e in range(2):
                    w1_codes[s, 2 * a + e] = codes[:, P * e : P * (e + 1)]
                    w1_scales[s, 2 * a + e] = scales[:, P * e : P * (e + 1)]

        picked_words = [sb.tile([P, S], U32, name=f"picked_words{s}", align_bytes=256) for s in range(PASSES)]

        def gather_words(s, j0, j1):
            nc.vector.tensor_copy(picked_words[s][:, j0:j1], xw[s][:].bitcast(U32).indirect(offs_t[:, j0 // 16 : j1 // 16]))

        def first_pass(acc, t, s, j0, j1):
            runs = [(j0, j1)] if j1 - j0 != 3 * P else [(j0, j0 + P), (j0 + P, j1)]
            for n, (c0, c1) in enumerate(runs):
                nc.tensor.matmul_mx(
                    out=acc[:, c0 - j0 : c1 - j0],
                    lhsT=w1_codes[s, t].bitcast(FP8X4),
                    lhsT_scale=w1_scales[s, t],
                    rhs=picked_words[s][:, c0:c1].bitcast(FP8X4),
                    rhs_scale=planes[s][4 * s : P, c0:c1],
                    start=(s == 0 and n == 0),
                    stop=(s == PASSES - 1 and n == len(runs) - 1),
                )

        pieces = [(1, 0, P), (0, 0, P), (0, P, S), (1, P, S), (2, 0, S), (3, 0, S)]
        accs = {}
        quantise_w1(0)
        gather_words(0, 0, S)
        for n, (t, j0, j1) in enumerate(pieces):
            accs[t, j0] = ps.tile([P, j1 - j0], F32, name=f"h{t}_{j0}", tag=f"bank{n}")
            first_pass(accs[t, j0], t, 0, j0, j1)
        quantise_w1(1)
        gather_words(1, 0, P)
        gather_words(1, P, S)
        for t, j0, j1 in pieces:
            first_pass(accs[t, j0], t, 1, j0, j1)

        skip_planes = skip.rearrange("(p t) v -> t p v", t=PACK)
        w2_raw = laid.tile([P, PACK, N], F32, name="w2raw", offset=4 * T, align_bytes=256)
        nc.sync.dma_start(w2_raw[:], w2.rearrange("(p t) n -> p t n", t=PACK))
        skip_t = []
        for t, slot in enumerate(["w1raw0", "xw0", "w1raw1", "x_late"]):
            if slot == "x_late":
                skip_t.append(laid.tile([P, U], F32, name=f"skip{t}", offset=0, align_bytes=256))
            else:
                skip_t.append(sb.tile([P, U], F32, name=f"skip{t}", tag=slot, align_bytes=256))
            nc.sync.dma_start(skip_t[t][:], skip_planes[t])

        hs = {}

        def relu(t, j0, j1, on_vector=False):
            hs[t, j0] = sb.tile([P, j1 - j0], F32, name=f"hs{t}_{j0}", tag=f"hs{t}_{j0}", align_bytes=256)
            if on_vector:
                nc.vector.tensor_scalar_max(hs[t, j0][:], accs[t, j0][:], 0.0)
            else:
                nc.scalar.activation(out=hs[t, j0][:], in_=accs[t, j0][:], func=ACT.Relu)

        def scatter_v(t, j0, j1, src):
            nc.vector.tensor_copy(window[t][:].indirect(cell_t[:, j0 // 16 : j1 // 16]), src)

        def scatter_s(t, j0, j1, src):
            nc.scalar.activation(out=window[t][:].indirect(cell_t[:, j0 // 16 : j1 // 16]), in_=src, func=ACT.Copy)

        def add_plane(t, v0=TURNED, v1=U):
            nc.vector.tensor_tensor(zb[:, t, v0 - TURNED : v1 - TURNED], window[t][:, v0:v1], skip_t[t][:, v0:v1], ALU.add)

        sums, back, grouped = {}, {}, {}

        def turn(u, source, e):
            for c in range(2):
                if (u, c) not in sums:
                    sums[u, c] = ps.tile([P, 2, 2, P], F32, name=f"sum{u}{c}", tag=f"bank{[5, 4, 0, 1][2 * u + c]}")
                for blk in range(2):
                    v0 = 2 * P * c + P * blk
                    nc.tensor.matmul(
                        sums[u, c][:, blk, e, :],
                        lhsT=source[2 * u + e][:, v0 : v0 + P],
                        rhs=ident[:],
                        is_transpose=True,
                        start=(source is skip_t and e == 0 and blk == 0),
                        stop=(source is window and e == 1 and blk == 1),
                    )

        def turn_back(u, c, copy):
            pairs = sb.tile([P, 2, P, 2], BF16, name=f"pairs{u}{c}", tag=f"pairs{u}{c}", align_bytes=256)
            copy(pairs[:], sums[u, c][:].rearrange("v b e p -> v b p e"))
            if u == 0:
                back[c] = ps.tile([P, 2, 2 * P], F32, name=f"back{c}", tag=f"bank{2 + c}")
            words = pairs[:].rearrange("v b p e -> v b (p e)").bitcast(F32)
            for blk in range(2):
                nc.tensor.transpose(back[c][:, u, P * blk : P * (blk + 1)], words[:, blk, :], ident[:])

        def join(c, copy):
            half, v0 = divmod(edges[c], 2 * P)
            width = edges[c + 1] - edges[c]
            grouped[c] = sb.tile([P, width, PACK], BF16, name=f"grouped{c}", align_bytes=256)
            words = grouped[c][:].rearrange("p v t -> p (v t)").bitcast(F32).rearrange("p (v u) -> p v u", u=2)
            copy(words, back[half][:, :, v0 : v0 + width].rearrange("p u v -> p v u"))

        relu(1, 0, P)
        relu(0, 0, P)
        scatter_v(0, 0, P, hs[0, 0][:])
        scatter_s(1, 0, P, hs[1, 0][:])
        relu(0, P, S, True)
        scatter_v(0, P, S, hs[0, P][:])
        relu(1, P, S)
        relu(2, 0, S)
        relu(3, 0, S)
        scatter_s(1, P, S, hs[1, P][:])
        scatter_v(2, SHARE, S, hs[2, 0][:, SHARE:S])
        w2_b = sb.tile([P, N, PACK], BF16, name="w2b", tag="hs0_128", align_bytes=256)
        nc.gpsimd.tensor_copy(w2_b[:], w2_raw[:].rearrange("p j n -> p n j"))
        turn(0, skip_t, 0)
        turn(0, skip_t, 1)
        turn(0, window, 0)
        turn(0, window, 1)
        turn(1, skip_t, 0)
        turn(1, skip_t, 1)
        turn_back(0, 0, dve)
        turn_back(0, 1, dve)
        zb = sb.tile([P, PACK, U - TURNED], BF16, name="zb", tag="pairs00", align_bytes=256)
        add_plane(0)
        add_plane(1)
        scatter_s(3, 0, S_HALF, hs[3, 0][:, 0:S_HALF])
        scatter_s(2, 0, SHARE, hs[2, 0][:, 0:SHARE])
        scatter_s(3, S_HALF, S, hs[3, 0][:, S_HALF:S])
        add_plane(2)
        turn(1, window, 0)
        turn(1, window, 1)
        edges = [0, 256, 384, 512, 768, 1024]
        chunk_cols = [slice(v0, v1) for v0, v1 in zip(edges, edges[1:])]
        accs_out = {}

        def weave(c, copy):
            grouped[c] = sb.tile([P, edges[c + 1] - edges[c], PACK], BF16, name=f"grouped{c}", align_bytes=256)
            copy(grouped[c][:].rearrange("p (c i) t -> p c t i", i=4), zb[:, :, edges[c] - TURNED : edges[c + 1] - TURNED].rearrange("p t (c i) -> p c t i", i=4))

        def second_layer(c):
            width = edges[c + 1] - edges[c]
            codes = sb.tile([P, width], U32, name=f"zc{c}", align_bytes=256)
            scales = sb.tile([P, width], U8, name=f"zs{c}", align_bytes=256)
            nc.vector.quantize_mx(out=codes[:].bitcast(FP8X4), scales=scales[:], in_=grouped[c][:].rearrange("p v t -> p (v t)"))
            accs_out[c] = ps.tile([P, width], F32, name=f"o{c}", tag=f"bank{[6, 7, 4, 1, 0][c]}")
            nc.tensor.matmul_mx(
                out=accs_out[c][:],
                lhsT=w2_codes[:].bitcast(FP8X4),
                lhsT_scale=w2_scales[:],
                rhs=codes[:].bitcast(FP8X4),
                rhs_scale=scales[:],
                start=True,
                stop=True,
            )

        def store(c, copy):
            res = sb.tile([P, edges[c + 1] - edges[c]], F32, name=f"res{c}", align_bytes=256)
            copy(res[:], accs_out[c][:])
            nc.sync.dma_start(out[:, chunk_cols[c]], res[:])

        add_plane(3, 512, 768)
        add_plane(3, 768, U)
        turn_back(1, 0, act)
        turn_back(1, 1, act)
        w2_codes = sb.tile([P, N], U32, name="w2c", tag="w1raw1", align_bytes=256)
        w2_scales = sb.tile([P, N], U8, name="w2s", align_bytes=256)
        nc.vector.quantize_mx(out=w2_codes[:].bitcast(FP8X4), scales=w2_scales[:], in_=w2_b[:].rearrange("p n j -> p (n j)"))
        weave(3, dve)
        weave(4, dve)
        for c in range(3):
            join(c, act)
        for c in (3, 4, 0, 1, 2):
            second_layer(c)
        for c, copy in ((3, act), (4, act), (0, act), (1, act), (2, dve)):
            store(c, copy)
